import numpy as np, ml_dtypes
CORES = [3,7,11,15,131,135,139,143]
N = 8
import mx_ref
BF = ml_dtypes.bfloat16
def gcols(t, e):
    v = np.concatenate([t.reshape(8, 16, -1, 4), np.zeros((8, 16, 1, 4), BF)], axis=2)
    return np.ascontiguousarray(np.stack([v[g][:, e[g]] for g in range(8)])).reshape(128, -1)
def pick(q, e):
    c = np.concatenate([q[0].reshape(128, -1, 4), np.zeros((128, 1, 4), np.uint8)], axis=1); s = np.concatenate([q[1], np.ones((16, 1), np.uint8)], axis=1)
    return (np.ascontiguousarray(c[:, e].reshape(128, -1)), np.ascontiguousarray(s[:, e]))
def join(*qs):
    return (np.concatenate([q[0] for q in qs], axis=1), np.concatenate([q[1] for q in qs], axis=1))
def put(q, e, v):
    c, s = q[0].reshape(128, -1, 4).copy(), q[1].copy(); c[:, e] = v[0].reshape(128, -1, 4); s[:, e] = v[1]
    return (c.reshape(128, -1), s)
def pk(c, s):
    return (np.ascontiguousarray(c), mx_ref.live(s))
def emit(q):
    return q[0], q[1]
def packed(v, rng):
    q = [mx_ref.quantize(np.ascontiguousarray(v[r])) for r in range(N)]
    return np.stack([a for a, b in q]), np.stack([mx_ref.plane(b, rng) for a, b in q])
def values_of_codes():
    e, c = np.zeros((128, 128, 4), np.float32), np.zeros((128, 2, 4), np.uint8)
    e[np.arange(128), np.arange(128), 0] = 1
    c[:127, :, 0] = np.arange(256).reshape(2, 128).T[:127]
    return mx_ref.matmul(mx_ref.quantize(e.reshape(128, 512).astype(BF)), (c.reshape(128, 8), np.full((16, 2), 127, np.uint8))).T.reshape(-1).astype(np.float64)
CODE_VALUE, SCALE_VALUE = values_of_codes(), 2.0 ** (np.arange(256) - 127.0)
def decode(q):
    return (CODE_VALUE[q[0]].reshape(16, 8, -1, 4) * SCALE_VALUE[q[1]][:, None, :, None] + 0.0).reshape(128, -1).astype(np.float32)
def f(rng, *shape):
    return mx_ref.flush((rng.standard_normal(shape, dtype=np.float32) * np.exp2(rng.integers(-2, 3, shape[:-1] + (1,)))).astype(BF))
def wide(rng, *shape, cols=0):
    v = rng.standard_normal(shape, dtype=np.float32) * np.exp2(rng.integers(-12, 13, shape)).astype(np.float32)
    if cols: v *= np.repeat(np.exp2(rng.integers(-cols, cols + 1, shape[:-2] + (1, shape[-1] // 4))) * (rng.random(shape[:-2] + (1, shape[-1] // 4)) > 0.0625), 4, axis=-1).astype(np.float32)
    return mx_ref.flush(v.astype(BF))
C, L, K = 256, 16, 160
MASKS = [4, 1, 2]
def big(v):
    v = v.astype(np.float32)
    v[np.abs(v) < np.float32(2.0 ** -16)] = 0
    return v.astype(BF)
def numbers_of(rng):
    return {"x": big(f(rng, N, 128, 4 * C)), "u": np.array(f(rng, N, 128, 512)), "v": np.array(f(rng, N, 128, 512))}
def layers(rng, still=[]):
    w = big(f(rng, N, 128, 2048)).reshape(N, 8, 16, 4, 8, 16, 4)
    for i in still:
        w[:, :, i] = 0
        w[:, :, :, :, :, i] = 0
    return w
def weights(rng, w):
    c, s = packed(np.ascontiguousarray(w).reshape(N, 128, 2048), rng)
    return {"wc": c, "ws": s}
def bare(u):
    u = u.reshape(N, 128, 128, 4)
    u[:, :, ::16] = 0
    u[:, :, 1::16] = 0
    return u
def back(x):
    return np.ascontiguousarray(x).astype(np.float32).reshape(N, 128, 4 * C).astype(BF)
def setup_inputs(rng):
    return {**numbers_of(rng), **weights(rng, layers(rng))}
def setup_inputs_ties(rng):
    d = numbers_of(rng)
    x = d["x"].astype(np.float32).reshape(N, 8, 16, C, 4)
    x[:, :, 0] = 0
    for b in range(2): x[:, :, 0, :, b] = np.minimum(rng.integers(0, 3, (N, 8, L, L)), rng.integers(0, 3, (N, 8, L, 1))).reshape(N, 8, C)
    u = bare(d["u"])
    o = rng.permutation(N)
    for r in range(N):
        k = 0.0 if r == o[0] else -1.0 if r == o[1] else 1.0
        for h in range(0, 128, 16):
            u[r, h, h, 0] = k
            u[r, h, h + 1, 1] = k
    return {"x": back(x), "u": u.reshape(N, 128, 512), "v": d["v"], **weights(rng, layers(rng, [0]))}
def setup_inputs_near(rng):
    d = numbers_of(rng)
    x = d["x"].astype(np.float32).reshape(N, 8, 16, C, 4)
    u = bare(d["u"])
    x[:, :, :2] = 0
    x[:, :, 8:] = 0
    o = rng.permutation(8) % 4
    for g in range(8):
        h, a = 16 * g, 2.0 ** -30 if o[g] >= 2 else 1.0
        if o[g] == 3:
            x[:, g, 10:12, :, 0] = 2.0 ** -29 * (1.0 + 0.125 * rng.integers(0, 6, (N, 2, C)))
            u[:, h + 10, h, 0] = -a
            u[:, h + 11, h + 1, 0] = -a
            continue
        i = h + 1 if o[g] == 1 else h
        x[:, g, 0, :, 0] = rng.integers(0, 2, (N, 1)) * 2.0 - 1.0
        x[:, g, 8:10] = ((rng.integers(0, 16, (N, 2, C))[..., None] >> np.arange(4)) & 1) * np.exp2(np.arange(4) - 23.0)
        x[:, g, 11, :, 0] = 2.0 ** -10
        u[:, h, i, 0] = a
        u[:, h + 11, i, 0] = a
        u[:, h + 8, h] = a
        u[:, h + 9, h + 1] = a
        if o[g] == 1: x[np.arange(N), g, 0, rng.integers(0, C, N), 0] = -2.0 ** 29
        else:
            for r in range(N):
                k = rng.permutation(L)
                x[r, g, 0, L * k[0]:L * k[0] + L, 0] = -2.0 ** 29
                x[r, g, 0, L * k[1] + rng.integers(0, L), 0] = 2.0 ** 29 * (rng.integers(0, 2) * 2.0 - 1.0)
    return {"x": back(x), "u": u.reshape(N, 128, 512), "v": d["v"], **weights(rng, layers(rng, [0, 1] + [8 + i for i in range(8)]))}
def setup_inputs_huge(rng):
    d = numbers_of(rng)
    x = -2.0 ** 30 * np.where(rng.random((N, 8, 16, C, 4)) < rng.random((N, 8, 1, C, 1)), 0.9375, 0.875)
    u = bare(d["u"])
    o = rng.permutation(8)
    for g in range(8):
        for b in range(2):
            for h in rng.permutation(8)[:8 if o[g] < 3 else 2]: u[:, 16 * h:16 * h + 16, 16 * g + b] = 2.0 ** 30 if o[g] % 2 == 0 else -2.0 ** 30
    w = np.zeros((N, 128, 4, 128, 4), np.float32)
    i = np.arange(128)
    for b in range(4): w[:, i, b, i, b] = -2
    return {"x": back(x), "u": u.reshape(N, 128, 512), "v": d["v"], **weights(rng, w.astype(BF))}
def setup_inputs_late(rng):
    d = numbers_of(rng)
    x = d["x"].astype(np.float32).reshape(N, 8, 16, C, 4)
    x[:, :, 8:] = (1.125 + 0.25 * rng.integers(0, 4, (N, 8, 8, C, 4))) * np.exp2(rng.integers(-1, 2, (N, 8, 8, C, 4))) * rng.choice([-1.0, 1.0], (N, 8, 8, C, 4))
    x[:, :, 8, :, 2:] = 1.96875 * 2.0 ** 13 * rng.choice([-1.0, 1.0], (8, 1, 1))
    u = bare(d["u"])
    for h in range(0, 128, 16):
        u[:, h, h, 0] = 1.0
        u[:, h, h + 1, 1] = 1.0
    s = MASKS[0]
    none = rng.permutation([r for r in range(N) if r < r ^ s])[:N // 4]
    for r in range(N):
        if min(r, r ^ s) in none: x[r, :, :8] = 0
        else:
            a = np.zeros((8, L, L), np.float32)
            np.put_along_axis(a, rng.integers(0, L, (8, L, 1)), np.exp2(np.argsort(rng.random((8, L, 1)), axis=1).astype(np.float32)), axis=2)
            x[r, :, 0] = 0
            x[r, :, 0, :, 0] = a.reshape(8, C)
            for h in range(0, 128, 16): u[r, h + 9, h + 1, 1] = 0.125
    w = layers(rng)
    w[:, :, 0] = 0
    w[:, :, 8] = 0
    for g in range(8):
        w[:, g, 8, 2:, g, 8, 2] = 16
        w[:, g, 8, 2:, g, 8, 3] = 15
    return {"x": back(x), "u": u.reshape(N, 128, 512), "v": d["v"], **weights(rng, w)}
def setup_inputs_spread(rng):
    d = setup_inputs(rng)
    d["x"] = big(wide(rng, N, 128, 4 * C, cols=6))
    return d
def check_inputs(d):
    b = []
    for k in ("x", "u", "v"):
        a = np.abs(d[k].astype(np.float32))
        if not (np.isfinite(a).all() and ((a == 0) | (a >= 2.0 ** -30) & (a <= 2.0 ** 30)).all()): b.append("a value of " + k)
    none, least, most = [emit(mx_ref.quantize(np.full((128, 16), k, np.float32).astype(BF)))[1][0, 0] for k in (0.0, 2.0 ** -30, 2.0 ** 30)]
    for r in range(N):
        if ((d["wc"][r] == 0x7F) | (d["wc"][r] == 0xFF)).any(): b.append("wc: a code that is no number")
        s = mx_ref.live(d["ws"][r])
        if ((s != none) & ((s < least) | (s > most))).any(): b.append("ws: a scale out of range")
    return b
def reference(x, u, v, wc, ws):
    qu = [mx_ref.quantize(u[r]) for r in range(N)]
    lay = [pk(wc[r], ws[r]) for r in range(N)]
    now = [x[r] for r in range(N)]
    for s in MASKS:
        q = [mx_ref.quantize(now[r]) for r in range(N)]
        t = [decode(q[r]) for r in range(N)]
        score = [mx_ref.matmul(qu[r], q[r]) + np.float32(0.0) for r in range(N)]
        made = []
        for r in range(N):
            d = r ^ s
            both = score[r][::16].reshape(8, L, 1, L) + score[d][1::16].reshape(8, 1, L, L)
            best, middle = np.max(both, axis=3).reshape(8, C), np.argmax(both, axis=3).reshape(8, C)
            e = np.argsort(-best, axis=1, kind="stable")[:, :K]
            m = np.take_along_axis(middle, e, axis=1)
            one = gcols(t[r].astype(BF), e // L * L + m).astype(np.float32)
            two = decode(mx_ref.quantize(gcols(t[d].astype(BF), e % L * L + m)))
            z = mx_ref.quantize(((one + two) * np.float32(0.5)).astype(BF))
            h = np.stack([mx_ref.matmul(pick(lay[r], np.arange(128 * b, 128 * b + 128)), z) * np.float32(0.03125) for b in range(4)], axis=2).reshape(8, 16, K, 4)
            n = t[r].reshape(8, 16, C, 4).copy()
            for g in range(8): n[g][:, e[g]] = n[g][:, e[g]] + h[g]
            made.append(n.reshape(128, 4 * C).astype(BF))
        now = made
    y = np.zeros((N, 128, C), np.float32)
    oc, osc = np.zeros((N, 128, 4 * C), np.uint8), np.zeros((N, 16, C), np.uint8)
    for r in range(N):
        q = mx_ref.quantize(now[r])
        y[r] = mx_ref.matmul(mx_ref.quantize(v[r]), q)
        oc[r], osc[r] = emit(q)
    return {"y": y, "oc": oc, "osc": osc}

@@ -1,0 +1,341 @@
+from concourse.mybir import dt, AluOpType, AxisListType, ActivationFunctionType
+
+A = AluOpType
+F = ActivationFunctionType
+MASKS = [4, 1, 2]
+C, K = 256, 160
+NLO, NV = 4, 6
+WID = [2 + (16 * t + 16 if t < NLO else C if t < NLO + NV else C - 16 * t - 16) for t in range(16)]
+CW = sum(WID)
+HW = 272
+X4, BF, F32 = "float8_e4m3fn_x4", "bfloat16", "float32"
+SCRATCH = {"ps": ("psum", [128, 4096], F32)}
+for _d, _l in (
+    (BF, dict(x0=1024, xs=1024, ut=512, vt=512, ones=516, eye=516, ti=1024, tp=1024, tb=1024, ah=4 * K, zt=4 * K, eqb=C, eqs=C,
+              cm=C, mrun=C, in4m=32, um=32, inv=C, vrow=C, ew=HW, tr=352, cmp=CW, cnt=CW, d0=CW, sg=16 * C, zn=32, d0e=C, d0m=C)),
+    (F32, dict(hs=4 * HW, ssb=288, stw=544, apre=C, sums=C, yy=C, run=C, in4=32, uu=32, in3=C, brep=C, qy=16, acc=16, rho=16,
+               wm=64, pf=24, d0x=C, cona=16, yo=C, bs0=16, bs1=16, bs2=16, bl0=16, bl1=16, bl2=16)),
+    (X4, dict(qu=128, qv=128, qw=512, qe=512, qz=K, qx0=C, qx1=C, qx2=C, qx3=C, qt0=C, qt1=C, qt2=C, ql0=C, ql1=C, ql2=C)),
+    ("uint8", dict(su=128, sv=128, sw=512, se=512, sz=K, sx0=C, sx1=C, sx2=C, sx3=C, st0=C, st1=C, st2=C, sl0=C, sl1=C, sl2=C)),
+    ("uint16", dict(offr=16, offab=32, offc=80)), ("int32", dict(ic=112, i256=C, pi=8)),
+):
+    for _n in _l:
+        SCRATCH[_n] = ("sbuf", [128, _l[_n]], _d)
+SEMAPHORES = ["nv", "ns", "nt", "ng", "lx", "lu", "lv", "lw", "out"] + [
+    "%s%d" % (n, r) for r in range(3) for n in ("arrs", "arrc", "snts", "sntc")]
+LB, L6, LAP, L4, LX, LQ, LV, LH, LE, LN = 0, 32, 48, 64, 66, 68, 70, 72, 74, 76
+
+
+def rank_program(g, core, T, topo):
+    rank = T.rank_of(core)
+    if rank is None:
+        return
+    Q = {"v": g.vector, "s": g.scalar, "t": g.tensor, "g": g, "y": g.sync}
+    own = {"v": "nv", "s": "ns", "t": "nt", "g": "ng"}
+    count = {n: 0 for n in SEMAPHORES}
+    seen = {q: {} for q in Q}
+    writer, readers = {}, {}
+
+    def wait(q, ev):
+        if seen[q].get(ev[0], 0) < ev[1]:
+            Q[q].wait_ge(T.sem[ev[0]], ev[1])
+            seen[q][ev[0]] = ev[1]
+
+    def before(q, rd, wr):
+        me = own.get(q)
+        need = {}
+        evs = []
+        for k in rd:
+            if k in writer:
+                evs.append(writer[k])
+            if k.startswith("ps"):
+                evs += [e for e in readers.get(k, []) if e[0] != me]
+        for k in wr:
+            evs += [e for e in [writer.get(k)] + readers.get(k, []) if e is not None]
+        for s, n in evs:
+            need[s] = max(need.get(s, 0), n)
+        for s in need:
+            wait(q, (s, need[s]))
+
+    def after(ev, rd, wr):
+        for k in rd:
+            readers.setdefault(k, []).append(ev)
+        for k in wr:
+            writer[k] = ev
+            readers[k] = []
+
+    def op(q, rd, wr, f):
+        before(q, rd, wr)
+        s = own[q]
+        f().then_inc(T.sem[s], 1)
+        count[s] += 1
+        after((s, count[s]), rd, wr)
+
+    def dma(q, s, rd, wr, out, in_):
+        before(q, rd, wr)
+        Q[q].dma_start(out, in_).then_inc(T.sem[s], 16)
+        count[s] += 16
+        after((s, count[s]), rd, wr)
+
+    V, S, PE = g.vector, g.scalar, g.tensor
+
+    def off(c, n):
+        return T.offc[:, c:c + n]
+
+    def bank(b, n):
+        return T.ps[:, 512 * b:512 * b + n]
+
+    def ts(out, in0, s1, s2, o0, o1, rd, wr):
+        if o1 is None:
+            op("v", rd, wr, lambda: V.tensor_scalar(out, in0, s1, None, o0))
+        else:
+            op("v", rd, wr, lambda: V.tensor_scalar(out, in0, s1, s2, o0, o1))
+
+    def tt(out, in0, in1, o, rd, wr):
+        op("v", rd, wr, lambda: V.tensor_tensor(out, in0, in1, o))
+
+    def cp(out, in_, rd, wr):
+        op("v", rd, wr, lambda: V.tensor_copy(out, in_))
+
+    def tp(out, in_, rd, wr):
+        op("v", rd, wr, lambda: V.transpose(out, in_))
+
+    def ms(ap, c, wr):
+        op("v", [], wr, lambda: V.memset(ap, c))
+
+    def scan(out, d0, d1, o0, o1, rd, wr):
+        op("v", rd, wr, lambda: V.tensor_tensor_scan(out, d0, d1, 0.0, o0, o1))
+
+    def qz(q, s, in_, rd, wr):
+        op("v", rd, wr, lambda: V.quantize_mx(q, s, in_))
+
+    def act(out, in_, f, rd, wr, **kw):
+        op("s", rd, wr, lambda: S.activation(out, in_, f, **kw))
+
+    def mm(b, n, w, ws, x, xs, rd):
+        op("t", rd, ["ps%d" % b], lambda: PE.matmul_mx(bank(b, n), w, ws, x, xs, True, True))
+
+    def unpack(b, to, q, s, key):
+        mm(to, C, T.qe[:, 128 * b:128 * b + 128], T.se[:, 128 * b:128 * b + 128], q[:], s[:], ["qe%d" % b, key])
+
+    def iota(out, pat, base, cm, wr):
+        op("g", [], wr, lambda: g.iota(out, pat, base, cm))
+
+    def pf(i, n=1):
+        return T.pf[:, i:i + n]
+
+    dma("y", "lx", [], ["x0"], T.x0[:], T.x[:])
+    dma("s", "lu", [], ["ut"], T.ut[:], T.u[:])
+    ms(T.ones[:], 1.0, ["ones"])
+    iota(T.pi[:, 0:1], [[1, 1]], 0, 1, ["p"])
+    op("g", ["ones"], ["eye"], lambda: g.affine_select(T.eye[:], T.ones[:], [[-1, 516]], A.is_equal, 0.0, 3, 4))
+    iota(T.ic[:, 0:16], [[1, 16]], 0, 0, ["ic0"])
+    iota(T.ic[:, 48:64], [[0, 8], [16, 2]], 0, 0, ["ic3"])
+    iota(T.i256[:], [[0, 16], [1, 16]], 0, 0, ["i256"])
+    iota(T.ic[:, 32:48], [[2, 8], [16, 2]], 0, 0, ["ic2"])
+    iota(T.ic[:, 80:82], [[0, 2]], 15, 16, ["ic5"])
+    iota(T.ic[:, 64:80], [[2, 8], [0, 2]], 0, 0, ["ic4"])
+    iota(T.ic[:, 96:96 + NLO], [[16, NLO]], WID[0], 0, ["w0"])
+    iota(T.ic[:, 96 + NLO:96 + NLO + NV], [[0, NV]], WID[NLO], 0, ["w1"])
+    iota(T.ic[:, 96 + NLO + NV:112], [[-16, 16 - NLO - NV]], WID[NLO + NV], 0, ["w2"])
+    for a in range(0, CW, 512):
+        b = min(a + 512, CW)
+        act(T.d0[:, a:b], T.ones[:, 0:b - a], F.Copy, ["ones"], ["d0_%d" % a])
+    d0keys = ["d0_%d" % a for a in range(0, CW, 512)]
+    ts(T.pi[:, 1:2], T.pi[:, 0:1], 15, None, A.bitwise_and, None, ["p"], ["p1"])
+    ts(T.pi[:, 2:3], T.pi[:, 0:1], 4, 1, A.logical_shift_right, A.bitwise_and, ["p"], ["p2"])
+    ts(T.pi[:, 3:4], T.pi[:, 0:1], 14, None, A.bitwise_and, None, ["p"], ["p3"])
+    ts(T.pi[:, 4:5], T.pi[:, 0:1], 1, None, A.bitwise_and, None, ["p"], ["p4"])
+    ts(T.pi[:, 5:6], T.pi[:, 0:1], 31, None, A.bitwise_and, None, ["p"], ["p5"])
+    ms(T.ssb[:, 0:16], 0.0, ["ssbe"])
+    ms(T.ssb[:, 272:288], 0.0, ["ssbe2"])
+    cp(pf(0, 6), T.pi[:, 0:6], ["p", "p1", "p2", "p3", "p4", "p5"], ["pf"])
+    R, H, R14, R0 = pf(1), pf(2), pf(3), pf(4)
+    ms(T.zn[:, 0:16], 0.0, ["zn0"])
+    tt(pf(6), R0, H, A.not_equal, ["pf"], ["par"])
+    ts(pf(7), R, H, 16.0, A.subtract, A.mult, ["pf"], ["pf7"])
+    ms(T.zn[:, 16:32], -1.0, ["zn1"])
+    ts(pf(8), pf(6), 272.0, pf(7), A.mult, A.add, ["par", "pf7"], ["pf8"])
+    for b in range(4):
+        qz(T.qe[:, 128 * b:128 * b + 128], T.se[:, 128 * b:128 * b + 128], T.eye[:, 3 - b:515 - b], ["eye"], ["qe%d" % b])
+    cp(off(LB, 16), T.ic[:, 0:16], ["ic0"], ["lb"])
+    ts(off(LAP, 16), T.ic[:, 48:64], pf(8), None, A.add, None, ["ic3", "pf8"], ["lap"])
+    cp(off(LQ, 1), T.pi[:, 5:6], ["p5"], ["lq"])
+    qz(T.qu[:], T.su[:], T.ut[:], ["ut"], ["qu"])
+
+    def late_constants():
+        ts(T.d0x[:], T.i256[:], 0.0, -1.0e29, A.is_equal, A.mult, ["i256"], ["d0x"])
+        ts(T.ic[:, 82:84], T.ic[:, 80:82], 255, None, A.bitwise_and, None, ["ic5"], ["ic6"])
+        ts(off(L6, 16), T.ic[:, 32:48], H, None, A.add, None, ["ic2", "pf"], ["l6"])
+        ts(pf(9), R0, 16.0, R14, A.mult, A.add, ["pf"], ["pf9"])
+        cp(off(L4, 2), T.ic[:, 82:84], ["ic6"], ["l4"])
+        ts(pf(10), R, 9.0, 16.0, A.min, A.mult, ["pf"], ["pf10"])
+        ts(T.wm[:, 0:16], T.ic[:, 0:16], R, None, A.is_lt, None, ["ic0", "pf"], ["wm0"])
+        ts(T.wm[:, 16:32], T.ic[:, 0:16], R, None, A.is_le, None, ["ic0", "pf"], ["wm1"])
+        ts(off(LV, 1), pf(9), H, None, A.add, None, ["pf9", "pf"], ["lv"])
+        ts(pf(11), pf(6), 176.0, pf(10), A.mult, A.add, ["par", "pf10"], ["pf11"])
+        tt(T.wm[:, 32:48], T.wm[:, 0:16], T.ic[:, 96:112], A.mult, ["wm0", "w0", "w1", "w2"], ["wm2"])
+        tt(T.wm[:, 48:64], T.wm[:, 16:32], T.ic[:, 96:112], A.mult, ["wm1", "w0", "w1", "w2"], ["wm3"])
+        ts(off(LX, 2), T.ic[:, 0:2], pf(11), None, A.add, None, ["ic0", "pf11"], ["lx"])
+        op("v", ["wm2"], ["pf16"], lambda: V.tensor_reduce(pf(16), T.wm[:, 32:48], AxisListType.X, A.add))
+        op("v", ["wm3"], ["pf17"], lambda: V.tensor_reduce(pf(17), T.wm[:, 48:64], AxisListType.X, A.add))
+        ts(T.cona[:], T.ic[:, 64:80], H, 16.0, A.add, A.mult, ["ic4", "pf"], ["cona"])
+        ts(pf(20), R, 16.0, None, A.mult, None, ["pf"], ["conb"])
+        cp(off(LH, 1), pf(16), ["pf16"], ["lh"])
+        ts(off(LN, 1), pf(16), 1.0, None, A.add, None, ["pf16"], ["ln"])
+        ts(off(LE, 1), pf(17), -1.0, None, A.add, None, ["pf17"], ["le"])
+        ts(T.d0e[:], T.i256[:], R, None, A.not_equal, None, ["i256", "pf"], ["d0e"])
+        ts(T.d0m[:], T.i256[:], 0.0, None, A.is_gt, None, ["i256"], ["d0m"])
+        cp(T.d0[:].indirect(off(LH, 1)), T.zn[:, 0:16], d0keys + ["lh", "zn0"], ["d0h"])
+        cp(T.cmp[:].indirect(off(LN, 1)), T.zn[:, 0:16], ["ln", "zn0"], ["cmpz"])
+        cp(T.d0[:].indirect(off(LN, 1)), T.zn[:, 16:32], d0keys + ["d0h", "ln", "zn1"], ["d0n"])
+        ms(T.ew[:, 0:16], 0.0, ["ewz"])
+        ms(T.inv[:], 0.0, ["invz"])
+        ms(T.acc[:], 0.0, ["accz"])
+        for b in range(4):
+            act(T.hs[:, HW * b:HW * b + HW], T.ones[:, 0:HW], F.Identity, ["ones"], ["hs%d" % b], scale=0.0)
+
+    d0all = d0keys + ["d0h", "d0n"]
+    x_ap, x_keys = T.x0[:], ["x0"]
+    for r in range(3):
+        mate = T.cores[rank ^ MASKS[r]]
+        rid, pid = topo.addr(mate, core)
+        eng = topo.engines(core, mate)[:8]
+        qx, sx, qt, st = T["qx%d" % r], T["sx%d" % r], T["qt%d" % r], T["st%d" % r]
+        ql, sl, bs, bl = T["ql%d" % r], T["sl%d" % r], T["bs%d" % r], T["bl%d" % r]
+
+        def send(out, in_, es, arr, snt, rd):
+            before("g", rd, [])
+            g.remote_dma(out, in_, T.sem[arr], T.sem[snt], pid, rid, sum(1 << e for e in es))
+            count[arr] += len(es)
+            count[snt] += len(es)
+
+        qz(qx[:], sx[:], x_ap, x_keys, ["qx%d" % r])
+        mm(4, C, T.qu[:], T.su[:], qx[:], sx[:], ["qu", "qx%d" % r])
+        mm(5, C, T.qu[:], T.su[:], qx[:], sx[:], ["qu", "qx%d" % r])
+        for b in (2, 0, 3, 1):
+            unpack(b, b, qx, sx, "qx%d" % r)
+        tp(T.stw[:, 0:256], bank(4, C), ["ps4"], ["stw0"])
+        cp(bs[:], T.stw[:, 1:256:16], ["stw0"], ["bs%d" % r])
+        send(bl[:], bs[:], eng, "arrs%d" % r, "snts%d" % r, ["bs%d" % r])
+        writer["bl"] = ("arrs%d" % r, count["arrs%d" % r])
+        act(T.ssb[:, 16:272], bank(5, C), F.Copy, ["ps5"], ["ssb"])
+        act(T.ti[:, 0:1024:4], bank(0, C), F.Copy, ["ps0"], ["ti0"])
+        cp(T.ti[:, 2:1024:4], bank(2, C), ["ps2"], ["ti2"])
+        tp(T.stw[:, 256:544], T.ssb[:], ["ssb", "ssbe", "ssbe2"], ["stw1"])
+        act(T.apre[:], T.stw[:].indirect(off(LAP, 16)), F.Copy, ["stw0", "stw1", "lap"], ["apre"])
+        cp(T.ti[:, 3:1024:4], bank(3, C), ["ps3"], ["ti3"])
+        act(T.ti[:, 1:1024:4], bank(1, C), F.Copy, ["ps1"], ["ti1"])
+        qz(qt[:], st[:], T.ti[:], ["ti%d" % b for b in range(4)], ["qt%d" % r])
+        send(ql[:].bitcast(dt.uint8), qt[:].bitcast(dt.uint8), eng, "arrc%d" % r, "sntc%d" % r, ["qt%d" % r])
+        send(sl[:], st[:], eng, "arrc%d" % r, "sntc%d" % r, ["qt%d" % r])
+        writer["ql"] = ("arrc%d" % r, count["arrc%d" % r])
+        if r == 0:
+            wait("y", ("sntc0", count["sntc0"]))
+            dma("y", "lw", [], [], T.qw[:].bitcast(dt.uint8), T.wc[:])
+            dma("y", "lw", [], ["qw"], T.sw[:], T.ws[:])
+            dma("y", "lv", [], ["vt"], T.vt[:], T.v[:])
+        for b in range(4):
+            act(T.tp[:, C * b:C * b + C], T.ti[:, b:1024:4], F.Copy, ["ti%d" % b], ["tp%d" % b])
+        if r == 0:
+            late_constants()
+        if r == 2:
+            qz(T.qv[:], T.sv[:], T.vt[:], ["vt"], ["qv"])
+        for b in range(4):
+            unpack(b, 4 + b, ql, sl, "ql")
+
+        tt(T.sums[:], bl[:].indirect(off(LB, 16)), T.apre[:], A.add, ["bl", "lb", "apre"], ["sums"])
+        tp(T.yy[:], T.sums[:], ["sums"], ["yy"])
+        scan(T.run[:], T.d0x[:], T.yy[:], A.add, A.max, ["d0x", "yy"], ["run"])
+        cp(T.in4[:], T.run[:].indirect(off(L4, 2)), ["run", "l4"], ["in4"])
+        tp(T.uu[:], T.in4[:], ["in4"], ["uu"])
+        act(T.qy[:], T.uu[:].indirect(off(LQ, 1)), F.Copy, ["uu", "lq"], ["qy"])
+        cp(T.in3[:], T.uu[:].indirect(off(L6, 16)), ["uu", "l6"], ["in3"])
+        tp(T.brep[:], T.in3[:], ["in3"], ["brep"])
+
+        jobs = [(t, 0, 16 * t + 16) for t in range(15, NLO + NV - 1, -1)] + [(t, 16 * t + 16, C) for t in range(NLO)]
+
+        def pass1(n):
+            t, a, b = jobs[n]
+            act(T.sg[:, C * t:C * t + b - a], T.brep[:, a:b], F.Sign, ["brep", "qy"], ["sg%d" % t], bias=T.qy[:, t:t + 1], scale=-1.0)
+
+        def pass2(n):
+            t, a, b = jobs[n]
+            w = T.sg[:, C * t:C * t + b - a]
+            if a == 0:
+                act(w, w, F.Sign, ["sg%d" % t, "accz"], ["sg%d" % t, "acc%d" % t], bias=1.0, scale=-1.0, accum_out=T.acc[:, t:t + 1])
+            else:
+                act(w, w, F.Relu, ["sg%d" % t, "accz"], ["sg%d" % t, "acc%d" % t], scale=-1.0, accum_out=T.acc[:, t:t + 1])
+
+        pass1(0)
+        for n in range(len(jobs)):
+            if n + 1 < len(jobs):
+                pass1(n + 1)
+            pass2(n)
+        for b in range(4):
+            act(T.tb[:, C * b:C * b + C], bank(4 + b, C), F.Copy, ["ps%d" % (4 + b)], ["tb%d" % b], scale=0.5)
+
+        comps = []
+        for t in range(16):
+            o = sum(WID[:t]) + 2
+            if t < NLO + NV:
+                comps.append((o, 0, 16 * t + 16, t, A.is_ge))
+                o += 16 * t + 16
+            if NLO <= t < 15:
+                comps.append((o, 16 * t + 16, C, t, A.is_gt))
+        ckeys = []
+
+        def comp(k):
+            for i in range(k):
+                if comps:
+                    o, a, b, t, c = comps.pop()
+                    ckeys.append("c%d" % o)
+                    ts(T.cmp[:, o:o + b - a], T.brep[:, a:b], T.qy[:, t:t + 1], None, c, None, ["brep", "qy"], [ckeys[-1]])
+
+        tt(T.cm[:], T.in4[:].indirect(off(LB, 16)), T.run[:], A.is_gt, ["in4", "run", "lb"], ["cm"])
+        tt(T.eqb[:], T.qy[:].indirect(off(LB, 16)), T.brep[:], A.is_equal, ["qy", "lb", "brep"], ["eqb"])
+        scan(T.mrun[:], T.d0m[:], T.cm[:], A.mult, A.add, ["d0m", "cm"], ["mrun"])
+        scan(T.eqs[:], T.d0e[:], T.eqb[:], A.mult, A.add, ["d0e", "eqb"], ["eqs"])
+        cp(T.in4m[:], T.mrun[:].indirect(off(L4, 2)), ["mrun", "l4"], ["in4m"])
+        cp(T.cmp[:].indirect(off(LH, 1)), T.eqs[:, 15:C:16], ["eqs", "lh", "cmpz"], ["heads"])
+        tp(T.um[:], T.in4m[:], ["in4m"], ["um"])
+        before("v", ["heads"], [])
+        comp(1)
+        tt(T.inv[:, 0:C:16], T.um[:].indirect(off(LV, 1)), T.cona[:], A.add, ["um", "lv", "cona", "invz"], ["inva"])
+        ts(T.inv[:, 1:C:16], T.um[:].indirect(off(LV, 1)), pf(20), None, A.add, None, ["um", "lv", "conb", "invz"], ["invb"])
+        comp(1)
+        tp(T.vrow[:], T.inv[:], ["inva", "invb", "invz"], ["vrow"])
+        comp(99)
+        scan(T.cnt[:], T.d0[:], T.cmp[:], A.mult, A.add, d0all + ckeys + ["heads"], ["cnt"])
+        tt(T.rho[:], T.cnt[:].indirect(off(LE, 1)), T.acc[:], A.add, ["cnt", "le", "accz"] + ["acc%d" % j[0] for j in jobs], ["rho"])
+        ts(T.offr[:], T.rho[:], 16.0, None, A.add, None, ["rho"], ["offr"])
+        cp(T.ew[:].indirect(T.offr[:]), T.vrow[:], ["offr", "vrow", "ewz"], ["ew"])
+        tp(T.tr[:, 0:160], T.ew[:, 16:176], ["ew"], ["tr0"])
+        tp(T.tr[:, 160:352], T.ew[:, 0:192], ["ew"], ["tr1"])
+        cp(T.offab[:], T.tr[:].indirect(off(LX, 2)), ["tr0", "tr1", "lx"], ["offab"])
+
+        for b in range(4):
+            act(T.ah[:, K * b:K * b + K], T.tp[:, C * b:C * b + C].indirect(T.offab[:, 0:10]), F.Copy,
+                ["tp%d" % b, "offab"], ["ah%d" % b], scale=0.5)
+            tt(T.zt[:, b:4 * K:4], T.tb[:, C * b:C * b + C].indirect(T.offab[:, 16:26]), T.ah[:, K * b:K * b + K], A.add,
+               ["tb%d" % b, "ah%d" % b, "offab"], ["zt%d" % b])
+        qz(T.qz[:], T.sz[:], T.zt[:], ["zt%d" % b for b in range(4)], ["qz"])
+        for b in range(4):
+            mm(b, K, T.qw[:, 128 * b:128 * b + 128], T.sw[:, 128 * b:128 * b + 128], T.qz[:], T.sz[:], ["qw", "qz"])
+            act(T.hs[:, HW * b + 16:HW * b + 16 + K], bank(b, K), F.Copy, ["ps%d" % b, "hs%d" % b], ["hs%d" % b], scale=0.03125)
+            tt(T.xs[:, b:1024:4], T.hs[:, HW * b:HW * b + HW].indirect(T.offr[:]), T.tp[:, C * b:C * b + C], A.add,
+               ["hs%d" % b, "offr", "tp%d" % b], ["xs%d" % b])
+        x_ap, x_keys = T.xs[:], ["xs%d" % b for b in range(4)]
+
+    qz(T.qx3[:], T.sx3[:], x_ap, x_keys, ["qx3"])
+    for h in range(2):
+        mm(4 + h, 128, T.qv[:], T.sv[:], T.qx3[:, 128 * h:128 * h + 128], T.sx3[:, 128 * h:128 * h + 128], ["qv", "qx3"])
+    dma("y", "out", ["qx3"], [], T.oc[:], T.qx3[:].bitcast(dt.uint8))
+    for k in range(4):
+        dma("y", "out", ["qx3"], [], T.osc[4 * k:4 * k + 4, :], T.sx3[32 * k:32 * k + 4, :])
+    cp(T.yo[:, 0:128], bank(4, 128), ["ps4"], ["yo0"])
+    act(T.yo[:, 128:256], bank(5, 128), F.Copy, ["ps5"], ["yo1"])
+    dma("s", "out", ["yo0", "yo1"], [], T.y[:], T.yo[:])
+    for s in SEMAPHORES:
+        if count[s]:
+            wait("y", (s, count[s]))

@@ -13,15 +13,15 @@ SCRATCH = {"ps": ("psum", [128, 4096], F32)}
 for _d, _l in (
     (BF, dict(x0=1024, xs=1024, ut=512, vt=512, ones=516, eye=516, ti=1024, tp=1024, tb=1024, ah=4 * K, zt=4 * K, eqb=C, eqs=C,
               cm=C, mrun=C, in4m=32, um=32, inv=C, vrow=C, ew=HW, tr=352, cmp=CW, cnt=CW, d0=CW, sg=16 * C, zn=32, d0e=C, d0m=C)),
-    (F32, dict(hs=4 * HW, ssb=288, stw=544, apre=C, sums=C, yy=C, run=C, in4=32, uu=32, in3=C, brep=C, qy=16, acc=16, rho=16,
-               wm=64, pf=24, d0x=C, cona=16, yo=C, bs0=16, bs1=16, bs2=16, bl0=16, bl1=16, bl2=16)),
+    (F32, dict(hs=4 * HW + 16, ssb=288, stw=544, apre=C, sums=C, yy=C, run=C, in4=32, uu=32, in3=C, brep=C, qy=16, acc=16, rho=16,
+               wm=64, pf=24, i256=C, sq=C, g3=C, d0x=C, cona=16, yo=C, bs0=16, bs1=16, bs2=16, bl0=16, bl1=16, bl2=16)),
     (X4, dict(qu=128, qv=128, qw=512, qe=512, qz=K, qx0=C, qx1=C, qx2=C, qx3=C, qt0=C, qt1=C, qt2=C, ql0=C, ql1=C, ql2=C)),
     ("uint8", dict(su=128, sv=128, sw=512, se=512, sz=K, sx0=C, sx1=C, sx2=C, sx3=C, st0=C, st1=C, st2=C, sl0=C, sl1=C, sl2=C)),
-    ("uint16", dict(offr=16, offab=32, offc=80)), ("int32", dict(ic=112, i256=C, pi=8)),
+    ("uint16", dict(offr=16, offab=32, offc=80)), ("int32", dict(ic=112, pi=8)),
 ):
     for _n in _l:
         SCRATCH[_n] = ("sbuf", [128, _l[_n]], _d)
-SEMAPHORES = ["nv", "ns", "nt", "ng", "lx", "lu", "lv", "lw", "out"] + [
+SEMAPHORES = ["nv", "ns", "nt", "ng", "lx", "lx1", "lu", "lv", "lw", "out"] + [
     "%s%d" % (n, r) for r in range(3) for n in ("arrs", "arrc", "snts", "sntc")]
 LB, L6, LAP, L4, LX, LQ, LV, LH, LE, LN = 0, 32, 48, 64, 66, 68, 70, 72, 74, 76
 
@@ -124,16 +124,17 @@ def rank_program(g, core, T, topo):
     def pf(i, n=1):
         return T.pf[:, i:i + n]
 
-    dma("y", "lx", [], ["x0"], T.x0[:], T.x[:])
+    dma("y", "lx", [], ["x00"], T.x0[:, 0:512], T.x[:, 0:512])
     dma("s", "lu", [], ["ut"], T.ut[:], T.u[:])
+    dma("y", "lx1", [], ["x01"], T.x0[:, 512:1024], T.x[:, 512:1024])
     ms(T.ones[:], 1.0, ["ones"])
     iota(T.pi[:, 0:1], [[1, 1]], 0, 1, ["p"])
     op("g", ["ones"], ["eye"], lambda: g.affine_select(T.eye[:], T.ones[:], [[-1, 516]], A.is_equal, 0.0, 3, 4))
     iota(T.ic[:, 0:16], [[1, 16]], 0, 0, ["ic0"])
     iota(T.ic[:, 48:64], [[0, 8], [16, 2]], 0, 0, ["ic3"])
-    iota(T.i256[:], [[0, 16], [1, 16]], 0, 0, ["i256"])
     iota(T.ic[:, 32:48], [[2, 8], [16, 2]], 0, 0, ["ic2"])
     iota(T.ic[:, 80:82], [[0, 2]], 15, 16, ["ic5"])
+    op("g", [], ["i256"], lambda: g.iota(T.i256[:], [[0, 16], [1, 16]], 0, 0, allow_small_or_imprecise_dtypes=True))
     iota(T.ic[:, 64:80], [[2, 8], [0, 2]], 0, 0, ["ic4"])
     iota(T.ic[:, 96:96 + NLO], [[16, NLO]], WID[0], 0, ["w0"])
     iota(T.ic[:, 96 + NLO:96 + NLO + NV], [[0, NV]], WID[NLO], 0, ["w1"])
@@ -161,42 +162,44 @@ def rank_program(g, core, T, topo):
     cp(off(LB, 16), T.ic[:, 0:16], ["ic0"], ["lb"])
     ts(off(LAP, 16), T.ic[:, 48:64], pf(8), None, A.add, None, ["ic3", "pf8"], ["lap"])
     cp(off(LQ, 1), T.pi[:, 5:6], ["p5"], ["lq"])
+    ts(T.ic[:, 82:84], T.ic[:, 80:82], 255, None, A.bitwise_and, None, ["ic5"], ["ic6"])
+    ts(off(L6, 16), T.ic[:, 32:48], H, None, A.add, None, ["ic2", "pf"], ["l6"])
+    cp(off(L4, 2), T.ic[:, 82:84], ["ic6"], ["l4"])
+    ms(T.acc[:], 0.0, ["accz"])
+    ms(T.ew[:, 0:16], 0.0, ["ewz"])
+    ms(T.hs[:, 0:16], 0.0, ["hq"])
+    act(T.d0m[:], T.i256[:], F.Sign, ["i256"], ["d0m"])
+    act(T.sq[:], T.i256[:], F.Square, ["i256", "pf"], ["sq"], bias=R, scale=-1.0)
+    act(T.d0x[:], T.d0m[:], F.Relu, ["d0m"], ["d0y"], bias=1.0, scale=-1.0)
     qz(T.qu[:], T.su[:], T.ut[:], ["ut"], ["qu"])
 
     def late_constants():
-        ts(T.d0x[:], T.i256[:], 0.0, -1.0e29, A.is_equal, A.mult, ["i256"], ["d0x"])
-        ts(T.ic[:, 82:84], T.ic[:, 80:82], 255, None, A.bitwise_and, None, ["ic5"], ["ic6"])
-        ts(off(L6, 16), T.ic[:, 32:48], H, None, A.add, None, ["ic2", "pf"], ["l6"])
-        ts(pf(9), R0, 16.0, R14, A.mult, A.add, ["pf"], ["pf9"])
-        cp(off(L4, 2), T.ic[:, 82:84], ["ic6"], ["l4"])
-        ts(pf(10), R, 9.0, 16.0, A.min, A.mult, ["pf"], ["pf10"])
+        act(T.d0x[:], T.d0x[:], F.Copy, ["d0y"], ["d0x"], scale=-1.0e29)
+        act(T.d0e[:], T.sq[:], F.Sign, ["sq"], ["d0e"])
         ts(T.wm[:, 0:16], T.ic[:, 0:16], R, None, A.is_lt, None, ["ic0", "pf"], ["wm0"])
         ts(T.wm[:, 16:32], T.ic[:, 0:16], R, None, A.is_le, None, ["ic0", "pf"], ["wm1"])
-        ts(off(LV, 1), pf(9), H, None, A.add, None, ["pf9", "pf"], ["lv"])
-        ts(pf(11), pf(6), 176.0, pf(10), A.mult, A.add, ["par", "pf10"], ["pf11"])
+        ts(pf(9), R0, 16.0, R14, A.mult, A.add, ["pf"], ["pf9"])
+        ts(pf(10), R, 9.0, 16.0, A.min, A.mult, ["pf"], ["pf10"])
         tt(T.wm[:, 32:48], T.wm[:, 0:16], T.ic[:, 96:112], A.mult, ["wm0", "w0", "w1", "w2"], ["wm2"])
         tt(T.wm[:, 48:64], T.wm[:, 16:32], T.ic[:, 96:112], A.mult, ["wm1", "w0", "w1", "w2"], ["wm3"])
-        ts(off(LX, 2), T.ic[:, 0:2], pf(11), None, A.add, None, ["ic0", "pf11"], ["lx"])
+        ts(off(LV, 1), pf(9), H, None, A.add, None, ["pf9", "pf"], ["lv"])
+        ts(pf(11), pf(6), 176.0, pf(10), A.mult, A.add, ["par", "pf10"], ["pf11"])
         op("v", ["wm2"], ["pf16"], lambda: V.tensor_reduce(pf(16), T.wm[:, 32:48], AxisListType.X, A.add))
         op("v", ["wm3"], ["pf17"], lambda: V.tensor_reduce(pf(17), T.wm[:, 48:64], AxisListType.X, A.add))
-        ts(T.cona[:], T.ic[:, 64:80], H, 16.0, A.add, A.mult, ["ic4", "pf"], ["cona"])
-        ts(pf(20), R, 16.0, None, A.mult, None, ["pf"], ["conb"])
+        ts(off(LX, 2), T.ic[:, 0:2], pf(11), None, A.add, None, ["ic0", "pf11"], ["lx"])
         cp(off(LH, 1), pf(16), ["pf16"], ["lh"])
         ts(off(LN, 1), pf(16), 1.0, None, A.add, None, ["pf16"], ["ln"])
         ts(off(LE, 1), pf(17), -1.0, None, A.add, None, ["pf17"], ["le"])
-        ts(T.d0e[:], T.i256[:], R, None, A.not_equal, None, ["i256", "pf"], ["d0e"])
-        ts(T.d0m[:], T.i256[:], 0.0, None, A.is_gt, None, ["i256"], ["d0m"])
         cp(T.d0[:].indirect(off(LH, 1)), T.zn[:, 0:16], d0keys + ["lh", "zn0"], ["d0h"])
         cp(T.cmp[:].indirect(off(LN, 1)), T.zn[:, 0:16], ["ln", "zn0"], ["cmpz"])
+        ts(T.cona[:], T.ic[:, 64:80], H, 16.0, A.add, A.mult, ["ic4", "pf"], ["cona"])
         cp(T.d0[:].indirect(off(LN, 1)), T.zn[:, 16:32], d0keys + ["d0h", "ln", "zn1"], ["d0n"])
-        ms(T.ew[:, 0:16], 0.0, ["ewz"])
+        ts(pf(20), R, 16.0, None, A.mult, None, ["pf"], ["conb"])
         ms(T.inv[:], 0.0, ["invz"])
-        ms(T.acc[:], 0.0, ["accz"])
-        for b in range(4):
-            act(T.hs[:, HW * b:HW * b + HW], T.ones[:, 0:HW], F.Identity, ["ones"], ["hs%d" % b], scale=0.0)
 
     d0all = d0keys + ["d0h", "d0n"]
-    x_ap, x_keys = T.x0[:], ["x0"]
+    hz = ["hq", "hz0", "hz1", "hz2", "hz3"]
+    xt, x_keys = T.x0, [["x00"], ["x01"]]
     for r in range(3):
         mate = T.cores[rank ^ MASKS[r]]
         rid, pid = topo.addr(mate, core)
@@ -210,22 +213,26 @@ def rank_program(g, core, T, topo):
             count[arr] += len(es)
             count[snt] += len(es)
 
-        qz(qx[:], sx[:], x_ap, x_keys, ["qx%d" % r])
-        mm(4, C, T.qu[:], T.su[:], qx[:], sx[:], ["qu", "qx%d" % r])
+        for h in range(2):
+            c = slice(128 * h, 128 * h + 128)
+            qz(qx[:, c], sx[:, c], xt[:, 512 * h:512 * h + 512], x_keys[h], ["qx%d%d" % (r, h)])
+            mm(6 + h, 128, T.qu[:], T.su[:], qx[:, c], sx[:, c], ["qu", "qx%d%d" % (r, h)])
+        writer["qx%d" % r] = writer["qx%d1" % r]
         mm(5, C, T.qu[:], T.su[:], qx[:], sx[:], ["qu", "qx%d" % r])
-        for b in (2, 0, 3, 1):
+        for b in (2, 0, 1, 3):
             unpack(b, b, qx, sx, "qx%d" % r)
-        tp(T.stw[:, 0:256], bank(4, C), ["ps4"], ["stw0"])
-        cp(bs[:], T.stw[:, 1:256:16], ["stw0"], ["bs%d" % r])
+        tp(T.stw[:, 0:128], bank(6, 128), ["ps6"], ["stwa"])
+        tp(T.stw[:, 128:256], bank(7, 128), ["ps7"], ["stw0"])
+        cp(bs[:], T.stw[:, 1:256:16], ["stwa", "stw0"], ["bs%d" % r])
         send(bl[:], bs[:], eng, "arrs%d" % r, "snts%d" % r, ["bs%d" % r])
         writer["bl"] = ("arrs%d" % r, count["arrs%d" % r])
         act(T.ssb[:, 16:272], bank(5, C), F.Copy, ["ps5"], ["ssb"])
         act(T.ti[:, 0:1024:4], bank(0, C), F.Copy, ["ps0"], ["ti0"])
+        act(T.ti[:, 1:1024:4], bank(1, C), F.Copy, ["ps1"], ["ti1"])
         cp(T.ti[:, 2:1024:4], bank(2, C), ["ps2"], ["ti2"])
         tp(T.stw[:, 256:544], T.ssb[:], ["ssb", "ssbe", "ssbe2"], ["stw1"])
-        act(T.apre[:], T.stw[:].indirect(off(LAP, 16)), F.Copy, ["stw0", "stw1", "lap"], ["apre"])
+        act(T.apre[:], T.stw[:].indirect(off(LAP, 16)), F.Copy, ["stwa", "stw0", "stw1", "lap"], ["apre"])
         cp(T.ti[:, 3:1024:4], bank(3, C), ["ps3"], ["ti3"])
-        act(T.ti[:, 1:1024:4], bank(1, C), F.Copy, ["ps1"], ["ti1"])
         qz(qt[:], st[:], T.ti[:], ["ti%d" % b for b in range(4)], ["qt%d" % r])
         send(ql[:].bitcast(dt.uint8), qt[:].bitcast(dt.uint8), eng, "arrc%d" % r, "sntc%d" % r, ["qt%d" % r])
         send(sl[:], st[:], eng, "arrc%d" % r, "sntc%d" % r, ["qt%d" % r])
@@ -235,12 +242,9 @@ def rank_program(g, core, T, topo):
             dma("y", "lw", [], [], T.qw[:].bitcast(dt.uint8), T.wc[:])
             dma("y", "lw", [], ["qw"], T.sw[:], T.ws[:])
             dma("y", "lv", [], ["vt"], T.vt[:], T.v[:])
+            late_constants()
         for b in range(4):
             act(T.tp[:, C * b:C * b + C], T.ti[:, b:1024:4], F.Copy, ["ti%d" % b], ["tp%d" % b])
-        if r == 0:
-            late_constants()
-        if r == 2:
-            qz(T.qv[:], T.sv[:], T.vt[:], ["vt"], ["qv"])
         for b in range(4):
             unpack(b, 4 + b, ql, sl, "ql")
 
@@ -249,8 +253,9 @@ def rank_program(g, core, T, topo):
         scan(T.run[:], T.d0x[:], T.yy[:], A.add, A.max, ["d0x", "yy"], ["run"])
         cp(T.in4[:], T.run[:].indirect(off(L4, 2)), ["run", "l4"], ["in4"])
         tp(T.uu[:], T.in4[:], ["in4"], ["uu"])
+        act(T.in3[:], T.uu[:].indirect(off(L6, 16)), F.Copy, ["uu", "l6"], ["in3"])
         act(T.qy[:], T.uu[:].indirect(off(LQ, 1)), F.Copy, ["uu", "lq"], ["qy"])
-        cp(T.in3[:], T.uu[:].indirect(off(L6, 16)), ["uu", "l6"], ["in3"])
+        tt(T.cm[:], T.in4[:].indirect(off(LB, 16)), T.run[:], A.is_gt, ["in4", "run", "lb"], ["cm"])
         tp(T.brep[:], T.in3[:], ["in3"], ["brep"])
 
         jobs = [(t, 0, 16 * t + 16) for t in range(15, NLO + NV - 1, -1)] + [(t, 16 * t + 16, C) for t in range(NLO)]
@@ -292,17 +297,15 @@ def rank_program(g, core, T, topo):
                     ckeys.append("c%d" % o)
                     ts(T.cmp[:, o:o + b - a], T.brep[:, a:b], T.qy[:, t:t + 1], None, c, None, ["brep", "qy"], [ckeys[-1]])
 
-        tt(T.cm[:], T.in4[:].indirect(off(LB, 16)), T.run[:], A.is_gt, ["in4", "run", "lb"], ["cm"])
-        tt(T.eqb[:], T.qy[:].indirect(off(LB, 16)), T.brep[:], A.is_equal, ["qy", "lb", "brep"], ["eqb"])
         scan(T.mrun[:], T.d0m[:], T.cm[:], A.mult, A.add, ["d0m", "cm"], ["mrun"])
-        scan(T.eqs[:], T.d0e[:], T.eqb[:], A.mult, A.add, ["d0e", "eqb"], ["eqs"])
+        tt(T.eqb[:], T.qy[:].indirect(off(LB, 16)), T.brep[:], A.is_equal, ["qy", "lb", "brep"], ["eqb"])
         cp(T.in4m[:], T.mrun[:].indirect(off(L4, 2)), ["mrun", "l4"], ["in4m"])
-        cp(T.cmp[:].indirect(off(LH, 1)), T.eqs[:, 15:C:16], ["eqs", "lh", "cmpz"], ["heads"])
+        scan(T.eqs[:], T.d0e[:], T.eqb[:], A.mult, A.add, ["d0e", "eqb"], ["eqs"])
         tp(T.um[:], T.in4m[:], ["in4m"], ["um"])
-        before("v", ["heads"], [])
-        comp(1)
+        cp(T.cmp[:].indirect(off(LH, 1)), T.eqs[:, 15:C:16], ["eqs", "lh", "cmpz"], ["heads"])
         tt(T.inv[:, 0:C:16], T.um[:].indirect(off(LV, 1)), T.cona[:], A.add, ["um", "lv", "cona", "invz"], ["inva"])
         ts(T.inv[:, 1:C:16], T.um[:].indirect(off(LV, 1)), pf(20), None, A.add, None, ["um", "lv", "conb", "invz"], ["invb"])
+        before("v", ["heads"], [])
         comp(1)
         tp(T.vrow[:], T.inv[:], ["inva", "invb", "invz"], ["vrow"])
         comp(99)
@@ -314,27 +317,39 @@ def rank_program(g, core, T, topo):
         tp(T.tr[:, 160:352], T.ew[:, 0:192], ["ew"], ["tr1"])
         cp(T.offab[:], T.tr[:].indirect(off(LX, 2)), ["tr0", "tr1", "lx"], ["offab"])
 
-        for b in range(4):
+        ts(T.ah[:, 0:K], T.tp[:, 0:C].indirect(T.offab[:, 0:10]), 0.5, None, A.mult, None, ["tp0", "offab"], ["ah0"])
+        for b in (1, 2, 3):
             act(T.ah[:, K * b:K * b + K], T.tp[:, C * b:C * b + C].indirect(T.offab[:, 0:10]), F.Copy,
                 ["tp%d" % b, "offab"], ["ah%d" % b], scale=0.5)
+        if r == 0:
+            for b in range(4):
+                act(T.hs[:, HW * b + 16 + K:HW * b + HW + 16], T.ones[:, 0:HW - K], F.Identity, ["ones"], ["hz%d" % b], scale=0.0)
+        for b in (1, 0, 2, 3):
             tt(T.zt[:, b:4 * K:4], T.tb[:, C * b:C * b + C].indirect(T.offab[:, 16:26]), T.ah[:, K * b:K * b + K], A.add,
                ["tb%d" % b, "ah%d" % b, "offab"], ["zt%d" % b])
         qz(T.qz[:], T.sz[:], T.zt[:], ["zt%d" % b for b in range(4)], ["qz"])
+        if r == 2:
+            qz(T.qv[:], T.sv[:], T.vt[:], ["vt"], ["qv"])
         for b in range(4):
-            mm(b, K, T.qw[:, 128 * b:128 * b + 128], T.sw[:, 128 * b:128 * b + 128], T.qz[:], T.sz[:], ["qw", "qz"])
-            act(T.hs[:, HW * b + 16:HW * b + 16 + K], bank(b, K), F.Copy, ["ps%d" % b, "hs%d" % b], ["hs%d" % b], scale=0.03125)
-            tt(T.xs[:, b:1024:4], T.hs[:, HW * b:HW * b + HW].indirect(T.offr[:]), T.tp[:, C * b:C * b + C], A.add,
-               ["hs%d" % b, "offr", "tp%d" % b], ["xs%d" % b])
-        x_ap, x_keys = T.xs[:], ["xs%d" % b for b in range(4)]
+            mm(4 + b, K, T.qw[:, 128 * b:128 * b + 128], T.sw[:, 128 * b:128 * b + 128], T.qz[:], T.sz[:], ["qw", "qz"])
+            act(T.hs[:, HW * b + 16:HW * b + 16 + K], bank(4 + b, K), F.Copy, ["ps%d" % (4 + b)], ["hs%d" % b], scale=0.03125)
+            if b < 3:
+                tt(T.xs[:, b:1024:4], T.hs[:, HW * b:HW * b + HW].indirect(T.offr[:]), T.tp[:, C * b:C * b + C], A.add,
+                   ["hs%d" % b, "offr", "tp%d" % b] + hz, ["xs%d" % b])
+        act(T.g3[:], T.hs[:, HW * 3:HW * 4].indirect(T.offr[:]), F.Copy, ["hs3", "offr"] + hz, ["g3"])
+        tt(T.xs[:, 3:1024:4], T.g3[:], bank(3, C), A.add, ["g3", "ps3"], ["xs3"])
+        xt, x_keys = T.xs, [["xs%d" % b for b in range(4)]] * 2
 
-    qz(T.qx3[:], T.sx3[:], x_ap, x_keys, ["qx3"])
     for h in range(2):
-        mm(4 + h, 128, T.qv[:], T.sv[:], T.qx3[:, 128 * h:128 * h + 128], T.sx3[:, 128 * h:128 * h + 128], ["qv", "qx3"])
+        c = slice(128 * h, 128 * h + 128)
+        qz(T.qx3[:, c], T.sx3[:, c], xt[:, 512 * h:512 * h + 512], x_keys[h], ["qx3%d" % h])
+        mm(4 + h, 128, T.qv[:], T.sv[:], T.qx3[:, c], T.sx3[:, c], ["qv", "qx3%d" % h])
+    writer["qx3"] = writer["qx31"]
     dma("y", "out", ["qx3"], [], T.oc[:], T.qx3[:].bitcast(dt.uint8))
     for k in range(4):
         dma("y", "out", ["qx3"], [], T.osc[4 * k:4 * k + 4, :], T.sx3[32 * k:32 * k + 4, :])
-    cp(T.yo[:, 0:128], bank(4, 128), ["ps4"], ["yo0"])
-    act(T.yo[:, 128:256], bank(5, 128), F.Copy, ["ps5"], ["yo1"])
+    act(T.yo[:, 0:128], bank(4, 128), F.Copy, ["ps4"], ["yo0"])
+    cp(T.yo[:, 128:256], bank(5, 128), ["ps5"], ["yo1"])
     dma("s", "out", ["yo0", "yo1"], [], T.y[:], T.yo[:])
     for s in SEMAPHORES:
         if count[s]:

@@ -4,26 +4,28 @@ A = AluOpType
 F = ActivationFunctionType
 MASKS = [4, 1, 2]
 C, K = 256, 160
-NLO, NV = 4, 6
-WID = [2 + (16 * t + 16 if t < NLO else C if t < NLO + NV else C - 16 * t - 16) for t in range(16)]
-CW = sum(WID)
+NLO, NV = 4, 8
+NH = NLO + NV
+WID = [2 + 16 * t + 16 if t < NLO else C // 2 if t < NH else 2 + C - 16 * t - 16 for t in range(16)]
+POS = [sum(WID[:t]) for t in range(17)]
+CW = POS[16]
 HW = 272
 X4, BF, F32 = "float8_e4m3fn_x4", "bfloat16", "float32"
 SCRATCH = {"ps": ("psum", [128, 4096], F32)}
 for _d, _l in (
     (BF, dict(x0=1024, xs=1024, ut=512, vt=512, ones=516, eye=516, ti=1024, tp=1024, tb=1024, ah=4 * K, zt=4 * K, eqb=C, eqs=C,
-              cm=C, mrun=C, in4m=32, um=32, inv=C, vrow=C, ew=HW, tr=352, cmp=CW, cnt=CW, d0=CW, sg=16 * C, zn=32, d0e=C, d0m=C)),
+              cm=C, mrun=C, mab=32, vrow=C, ew=HW, tr=352, cmp=CW, cmf=C * NV, cnt=CW, d0=CW, sg=16 * C, zn=16, d0e=C, d0m=C)),
     (F32, dict(hs=4 * HW + 16, ssb=288, stw=544, apre=C, sums=C, yy=C, run=C, in4=32, uu=32, in3=C, brep=C, qy=16, acc=16, rho=16,
-               wm=64, pf=24, i256=C, sq=C, g3=C, d0x=C, cona=16, yo=C, bs0=16, bs1=16, bs2=16, bl0=16, bl1=16, bl2=16)),
+               wm=64, pf=24, i256=C, sq=C, g3=C, d0x=C, cab=32, yo=C, bs0=16, bs1=16, bs2=16, bl0=16, bl1=16, bl2=16)),
     (X4, dict(qu=128, qv=128, qw=512, qe=512, qz=K, qx0=C, qx1=C, qx2=C, qx3=C, qt0=C, qt1=C, qt2=C, ql0=C, ql1=C, ql2=C)),
     ("uint8", dict(su=128, sv=128, sw=512, se=512, sz=K, sx0=C, sx1=C, sx2=C, sx3=C, st0=C, st1=C, st2=C, sl0=C, sl1=C, sl2=C)),
     ("uint16", dict(offr=16, offab=32, offc=80)), ("int32", dict(ic=112, pi=8)),
 ):
     for _n in _l:
         SCRATCH[_n] = ("sbuf", [128, _l[_n]], _d)
-SEMAPHORES = ["nv", "ns", "nt", "ng", "lx", "lx1", "lu", "lv", "lw", "out"] + [
+SEMAPHORES = ["nv", "ns", "nt", "ng", "lx", "lx1", "lu", "lv", "lw", "lm", "out"] + [
     "%s%d" % (n, r) for r in range(3) for n in ("arrs", "arrc", "snts", "sntc")]
-LB, L6, LAP, L4, LX, LQ, LV, LH, LE, LN = 0, 32, 48, 64, 66, 68, 70, 72, 74, 76
+LB, L6, LAP, L4, LX, LQ, LH, LE, LN = 0, 32, 48, 64, 66, 68, 72, 74, 76
 
 
 def rank_program(g, core, T, topo):
@@ -36,10 +38,14 @@ def rank_program(g, core, T, topo):
     seen = {q: {} for q in Q}
     writer, readers = {}, {}
 
+    known = {}
+
     def wait(q, ev):
         if seen[q].get(ev[0], 0) < ev[1]:
             Q[q].wait_ge(T.sem[ev[0]], ev[1])
             seen[q][ev[0]] = ev[1]
+            for s, n in known.get(ev, {}).items():
+                seen[q][s] = max(seen[q].get(s, 0), n)
 
     def before(q, rd, wr):
         me = own.get(q)
@@ -55,9 +61,11 @@ def rank_program(g, core, T, topo):
         for s, n in evs:
             need[s] = max(need.get(s, 0), n)
         for s in need:
-            wait(q, (s, need[s]))
+            if not any(known.get((o, need[o]), {}).get(s, 0) >= need[s] for o in need if o != s):
+                wait(q, (s, need[s]))
 
-    def after(ev, rd, wr):
+    def after(q, ev, rd, wr):
+        known[ev] = dict(seen[q])
         for k in rd:
             readers.setdefault(k, []).append(ev)
         for k in wr:
@@ -69,13 +77,13 @@ def rank_program(g, core, T, topo):
         s = own[q]
         f().then_inc(T.sem[s], 1)
         count[s] += 1
-        after((s, count[s]), rd, wr)
+        after(q, (s, count[s]), rd, wr)
 
     def dma(q, s, rd, wr, out, in_):
         before(q, rd, wr)
         Q[q].dma_start(out, in_).then_inc(T.sem[s], 16)
         count[s] += 16
-        after((s, count[s]), rd, wr)
+        after(q, (s, count[s]), rd, wr)
 
     V, S, PE = g.vector, g.scalar, g.tensor
 
@@ -103,8 +111,8 @@ def rank_program(g, core, T, topo):
     def ms(ap, c, wr):
         op("v", [], wr, lambda: V.memset(ap, c))
 
-    def scan(out, d0, d1, o0, o1, rd, wr):
-        op("v", rd, wr, lambda: V.tensor_tensor_scan(out, d0, d1, 0.0, o0, o1))
+    def scan(out, d0, d1, o0, o1, rd, wr, first=0.0):
+        op("v", rd, wr, lambda: V.tensor_tensor_scan(out, d0, d1, first, o0, o1))
 
     def qz(q, s, in_, rd, wr):
         op("v", rd, wr, lambda: V.quantize_mx(q, s, in_))
@@ -129,45 +137,47 @@ def rank_program(g, core, T, topo):
     dma("y", "lx1", [], ["x01"], T.x0[:, 512:1024], T.x[:, 512:1024])
     ms(T.ones[:], 1.0, ["ones"])
     iota(T.pi[:, 0:1], [[1, 1]], 0, 1, ["p"])
-    op("g", ["ones"], ["eye"], lambda: g.affine_select(T.eye[:], T.ones[:], [[-1, 516]], A.is_equal, 0.0, 3, 4))
     iota(T.ic[:, 0:16], [[1, 16]], 0, 0, ["ic0"])
+    op("g", ["ones"], ["eye"], lambda: g.affine_select(T.eye[:], T.ones[:], [[-1, 516]], A.is_equal, 0.0, 3, 4))
     iota(T.ic[:, 48:64], [[0, 8], [16, 2]], 0, 0, ["ic3"])
     iota(T.ic[:, 32:48], [[2, 8], [16, 2]], 0, 0, ["ic2"])
     iota(T.ic[:, 80:82], [[0, 2]], 15, 16, ["ic5"])
     op("g", [], ["i256"], lambda: g.iota(T.i256[:], [[0, 16], [1, 16]], 0, 0, allow_small_or_imprecise_dtypes=True))
-    iota(T.ic[:, 64:80], [[2, 8], [0, 2]], 0, 0, ["ic4"])
     iota(T.ic[:, 96:96 + NLO], [[16, NLO]], WID[0], 0, ["w0"])
-    iota(T.ic[:, 96 + NLO:96 + NLO + NV], [[0, NV]], WID[NLO], 0, ["w1"])
-    iota(T.ic[:, 96 + NLO + NV:112], [[-16, 16 - NLO - NV]], WID[NLO + NV], 0, ["w2"])
+    iota(T.ic[:, 96 + NLO:96 + NH], [[0, NV]], WID[NLO], 0, ["w1"])
+    iota(T.ic[:, 96 + NH:112], [[-16, 16 - NH]], WID[NH], 0, ["w2"])
     for a in range(0, CW, 512):
         b = min(a + 512, CW)
         act(T.d0[:, a:b], T.ones[:, 0:b - a], F.Copy, ["ones"], ["d0_%d" % a])
     d0keys = ["d0_%d" % a for a in range(0, CW, 512)]
     ts(T.pi[:, 1:2], T.pi[:, 0:1], 15, None, A.bitwise_and, None, ["p"], ["p1"])
     ts(T.pi[:, 2:3], T.pi[:, 0:1], 4, 1, A.logical_shift_right, A.bitwise_and, ["p"], ["p2"])
-    ts(T.pi[:, 3:4], T.pi[:, 0:1], 14, None, A.bitwise_and, None, ["p"], ["p3"])
-    ts(T.pi[:, 4:5], T.pi[:, 0:1], 1, None, A.bitwise_and, None, ["p"], ["p4"])
-    ts(T.pi[:, 5:6], T.pi[:, 0:1], 31, None, A.bitwise_and, None, ["p"], ["p5"])
+    ts(T.pi[:, 3:4], T.pi[:, 0:1], 1, None, A.bitwise_and, None, ["p"], ["p3"])
+    ts(T.pi[:, 4:5], T.pi[:, 0:1], 31, None, A.bitwise_and, None, ["p"], ["p4"])
     ms(T.ssb[:, 0:16], 0.0, ["ssbe"])
     ms(T.ssb[:, 272:288], 0.0, ["ssbe2"])
-    cp(pf(0, 6), T.pi[:, 0:6], ["p", "p1", "p2", "p3", "p4", "p5"], ["pf"])
-    R, H, R14, R0 = pf(1), pf(2), pf(3), pf(4)
-    ms(T.zn[:, 0:16], 0.0, ["zn0"])
+    cp(pf(0, 5), T.pi[:, 0:5], ["p", "p1", "p2", "p3", "p4"], ["pf"])
+    R, H, R0 = pf(1), pf(2), pf(3)
+    ms(T.zn[:], 0.0, ["zn0"])
     tt(pf(6), R0, H, A.not_equal, ["pf"], ["par"])
     ts(pf(7), R, H, 16.0, A.subtract, A.mult, ["pf"], ["pf7"])
-    ms(T.zn[:, 16:32], -1.0, ["zn1"])
+    ms(T.vrow[:], 0.0, ["vrow"])
     ts(pf(8), pf(6), 272.0, pf(7), A.mult, A.add, ["par", "pf7"], ["pf8"])
-    for b in range(4):
-        qz(T.qe[:, 128 * b:128 * b + 128], T.se[:, 128 * b:128 * b + 128], T.eye[:, 3 - b:515 - b], ["eye"], ["qe%d" % b])
-    cp(off(LB, 16), T.ic[:, 0:16], ["ic0"], ["lb"])
-    ts(off(LAP, 16), T.ic[:, 48:64], pf(8), None, A.add, None, ["ic3", "pf8"], ["lap"])
-    cp(off(LQ, 1), T.pi[:, 5:6], ["p5"], ["lq"])
-    ts(T.ic[:, 82:84], T.ic[:, 80:82], 255, None, A.bitwise_and, None, ["ic5"], ["ic6"])
-    ts(off(L6, 16), T.ic[:, 32:48], H, None, A.add, None, ["ic2", "pf"], ["l6"])
-    cp(off(L4, 2), T.ic[:, 82:84], ["ic6"], ["l4"])
     ms(T.acc[:], 0.0, ["accz"])
     ms(T.ew[:, 0:16], 0.0, ["ewz"])
     ms(T.hs[:, 0:16], 0.0, ["hq"])
+    cp(off(LQ, 1), T.pi[:, 4:5], ["p4"], ["lq"])
+    ts(pf(10), R, 9.0, 16.0, A.min, A.mult, ["pf"], ["pf10"])
+    ts(pf(20), R, 16.0, None, A.mult, None, ["pf"], ["pf20"])
+    cp(off(LB, 16), T.ic[:, 0:16], ["ic0"], ["lb"])
+    ts(T.wm[:, 0:16], T.ic[:, 0:16], R, None, A.is_lt, None, ["ic0", "pf"], ["wm0"])
+    ts(pf(11), pf(6), 176.0, pf(10), A.mult, A.add, ["par", "pf10"], ["pf11"])
+    ts(T.wm[:, 16:32], T.ic[:, 0:16], R, None, A.is_le, None, ["ic0", "pf"], ["wm1"])
+    ts(T.cab[:, 0:16], T.zn[:], pf(20), None, A.add, None, ["zn0", "pf20"], ["cona"])
+    ts(T.cab[:, 16:32], T.ic[:, 0:16], 16.0, None, A.mult, None, ["ic0"], ["conb"])
+    ts(off(LX, 2), T.ic[:, 0:2], pf(11), None, A.add, None, ["ic0", "pf11"], ["lx"])
+    for b in range(4):
+        qz(T.qe[:, 128 * b:128 * b + 128], T.se[:, 128 * b:128 * b + 128], T.eye[:, 3 - b:515 - b], ["eye"], ["qe%d" % b])
     act(T.d0m[:], T.i256[:], F.Sign, ["i256"], ["d0m"])
     act(T.sq[:], T.i256[:], F.Square, ["i256", "pf"], ["sq"], bias=R, scale=-1.0)
     act(T.d0x[:], T.d0m[:], F.Relu, ["d0m"], ["d0y"], bias=1.0, scale=-1.0)
@@ -176,34 +186,27 @@ def rank_program(g, core, T, topo):
     def late_constants():
         act(T.d0x[:], T.d0x[:], F.Copy, ["d0y"], ["d0x"], scale=-1.0e29)
         act(T.d0e[:], T.sq[:], F.Sign, ["sq"], ["d0e"])
-        ts(T.wm[:, 0:16], T.ic[:, 0:16], R, None, A.is_lt, None, ["ic0", "pf"], ["wm0"])
-        ts(T.wm[:, 16:32], T.ic[:, 0:16], R, None, A.is_le, None, ["ic0", "pf"], ["wm1"])
-        ts(pf(9), R0, 16.0, R14, A.mult, A.add, ["pf"], ["pf9"])
-        ts(pf(10), R, 9.0, 16.0, A.min, A.mult, ["pf"], ["pf10"])
         tt(T.wm[:, 32:48], T.wm[:, 0:16], T.ic[:, 96:112], A.mult, ["wm0", "w0", "w1", "w2"], ["wm2"])
         tt(T.wm[:, 48:64], T.wm[:, 16:32], T.ic[:, 96:112], A.mult, ["wm1", "w0", "w1", "w2"], ["wm3"])
-        ts(off(LV, 1), pf(9), H, None, A.add, None, ["pf9", "pf"], ["lv"])
-        ts(pf(11), pf(6), 176.0, pf(10), A.mult, A.add, ["par", "pf10"], ["pf11"])
+        ts(T.ic[:, 82:84], T.ic[:, 80:82], 255, None, A.bitwise_and, None, ["ic5"], ["ic6"])
         op("v", ["wm2"], ["pf16"], lambda: V.tensor_reduce(pf(16), T.wm[:, 32:48], AxisListType.X, A.add))
         op("v", ["wm3"], ["pf17"], lambda: V.tensor_reduce(pf(17), T.wm[:, 48:64], AxisListType.X, A.add))
-        ts(off(LX, 2), T.ic[:, 0:2], pf(11), None, A.add, None, ["ic0", "pf11"], ["lx"])
+        ts(off(L6, 16), T.ic[:, 32:48], H, None, A.add, None, ["ic2", "pf"], ["l6"])
+        cp(off(L4, 2), T.ic[:, 82:84], ["ic6"], ["l4"])
         cp(off(LH, 1), pf(16), ["pf16"], ["lh"])
         ts(off(LN, 1), pf(16), 1.0, None, A.add, None, ["pf16"], ["ln"])
         ts(off(LE, 1), pf(17), -1.0, None, A.add, None, ["pf17"], ["le"])
-        cp(T.d0[:].indirect(off(LH, 1)), T.zn[:, 0:16], d0keys + ["lh", "zn0"], ["d0h"])
-        cp(T.cmp[:].indirect(off(LN, 1)), T.zn[:, 0:16], ["ln", "zn0"], ["cmpz"])
-        ts(T.cona[:], T.ic[:, 64:80], H, 16.0, A.add, A.mult, ["ic4", "pf"], ["cona"])
-        cp(T.d0[:].indirect(off(LN, 1)), T.zn[:, 16:32], d0keys + ["d0h", "ln", "zn1"], ["d0n"])
-        ts(pf(20), R, 16.0, None, A.mult, None, ["pf"], ["conb"])
-        ms(T.inv[:], 0.0, ["invz"])
+        cp(T.d0[:].indirect(off(LH, 1)), T.zn[:], d0keys + ["lh", "zn0"], ["d0h"])
+        cp(T.cmp[:].indirect(off(LN, 1)), T.zn[:], ["ln", "zn0"], ["cmpz"])
 
-    d0all = d0keys + ["d0h", "d0n"]
+    d0all = d0keys + ["d0h"]
     hz = ["hq", "hz0", "hz1", "hz2", "hz3"]
+    halves = [slice(0, 128), slice(128, C)]
     xt, x_keys = T.x0, [["x00"], ["x01"]]
     for r in range(3):
         mate = T.cores[rank ^ MASKS[r]]
         rid, pid = topo.addr(mate, core)
-        eng = topo.engines(core, mate)[:8]
+        eng = topo.engines(core, mate)
         qx, sx, qt, st = T["qx%d" % r], T["sx%d" % r], T["qt%d" % r], T["st%d" % r]
         ql, sl, bs, bl = T["ql%d" % r], T["sl%d" % r], T["bs%d" % r], T["bl%d" % r]
 
@@ -214,51 +217,63 @@ def rank_program(g, core, T, topo):
             count[snt] += len(es)
 
         for h in range(2):
-            c = slice(128 * h, 128 * h + 128)
+            c = halves[h]
             qz(qx[:, c], sx[:, c], xt[:, 512 * h:512 * h + 512], x_keys[h], ["qx%d%d" % (r, h)])
             mm(6 + h, 128, T.qu[:], T.su[:], qx[:, c], sx[:, c], ["qu", "qx%d%d" % (r, h)])
         writer["qx%d" % r] = writer["qx%d1" % r]
-        mm(5, C, T.qu[:], T.su[:], qx[:], sx[:], ["qu", "qx%d" % r])
         for b in (2, 0, 1, 3):
             unpack(b, b, qx, sx, "qx%d" % r)
-        tp(T.stw[:, 0:128], bank(6, 128), ["ps6"], ["stwa"])
-        tp(T.stw[:, 128:256], bank(7, 128), ["ps7"], ["stw0"])
-        cp(bs[:], T.stw[:, 1:256:16], ["stwa", "stw0"], ["bs%d" % r])
+        for h in range(2):
+            tp(T.stw[:, halves[h]], bank(6 + h, 128), ["ps%d" % (6 + h)], ["stw%d" % h])
+        cp(bs[:], T.stw[:, 1:256:16], ["stw0", "stw1"], ["bs%d" % r])
         send(bl[:], bs[:], eng, "arrs%d" % r, "snts%d" % r, ["bs%d" % r])
         writer["bl"] = ("arrs%d" % r, count["arrs%d" % r])
-        act(T.ssb[:, 16:272], bank(5, C), F.Copy, ["ps5"], ["ssb"])
-        act(T.ti[:, 0:1024:4], bank(0, C), F.Copy, ["ps0"], ["ti0"])
-        act(T.ti[:, 1:1024:4], bank(1, C), F.Copy, ["ps1"], ["ti1"])
-        cp(T.ti[:, 2:1024:4], bank(2, C), ["ps2"], ["ti2"])
-        tp(T.stw[:, 256:544], T.ssb[:], ["ssb", "ssbe", "ssbe2"], ["stw1"])
-        act(T.apre[:], T.stw[:].indirect(off(LAP, 16)), F.Copy, ["stwa", "stw0", "stw1", "lap"], ["apre"])
-        cp(T.ti[:, 3:1024:4], bank(3, C), ["ps3"], ["ti3"])
-        qz(qt[:], st[:], T.ti[:], ["ti%d" % b for b in range(4)], ["qt%d" % r])
-        send(ql[:].bitcast(dt.uint8), qt[:].bitcast(dt.uint8), eng, "arrc%d" % r, "sntc%d" % r, ["qt%d" % r])
-        send(sl[:], st[:], eng, "arrc%d" % r, "sntc%d" % r, ["qt%d" % r])
-        writer["ql"] = ("arrc%d" % r, count["arrc%d" % r])
         if r == 0:
-            wait("y", ("sntc0", count["sntc0"]))
-            dma("y", "lw", [], [], T.qw[:].bitcast(dt.uint8), T.wc[:])
-            dma("y", "lw", [], ["qw"], T.sw[:], T.ws[:])
-            dma("y", "lv", [], ["vt"], T.vt[:], T.v[:])
-            late_constants()
-        for b in range(4):
-            act(T.tp[:, C * b:C * b + C], T.ti[:, b:1024:4], F.Copy, ["ti%d" % b], ["tp%d" % b])
-        for b in range(4):
-            unpack(b, 4 + b, ql, sl, "ql")
+            ts(off(LAP, 16), T.ic[:, 48:64], pf(8), None, A.add, None, ["ic3", "pf8"], ["lap"])
+        for h in range(2):
+            act(T.ssb[:, 16 + 128 * h:144 + 128 * h], bank(6 + h, 128), F.Copy, ["ps%d" % (6 + h)], ["ssb%d" % h])
+        tp(T.stw[:, 256:544], T.ssb[:], ["ssb0", "ssb1", "ssbe", "ssbe2"], ["stw2"])
+        act(T.apre[:], T.stw[:].indirect(off(LAP, 16)), F.Copy, ["stw0", "stw1", "stw2", "lap"], ["apre"])
+        for b in (2, 0):
+            cp(T.ti[:, b:1024:4], bank(b, C), ["ps%d" % b], ["ti%d" % b])
+        for b in (1, 3):
+            act(T.ti[:, b:1024:4], bank(b, C), F.Copy, ["ps%d" % b], ["ti%d" % b])
 
-        tt(T.sums[:], bl[:].indirect(off(LB, 16)), T.apre[:], A.add, ["bl", "lb", "apre"], ["sums"])
-        tp(T.yy[:], T.sums[:], ["sums"], ["yy"])
-        scan(T.run[:], T.d0x[:], T.yy[:], A.add, A.max, ["d0x", "yy"], ["run"])
-        cp(T.in4[:], T.run[:].indirect(off(L4, 2)), ["run", "l4"], ["in4"])
+        def requantise(h):
+            qz(qt[:, halves[h]], st[:, halves[h]], T.ti[:, 512 * h:512 * h + 512], ["ti%d" % b for b in range(4)], ["qt%d%d" % (r, h)])
+            if h == 1:
+                keys = ["qt%d0" % r, "qt%d1" % r]
+                send(ql[:].bitcast(dt.uint8), qt[:].bitcast(dt.uint8), eng, "arrc%d" % r, "sntc%d" % r, keys)
+                send(sl[:], st[:], eng, "arrc%d" % r, "sntc%d" % r, keys)
+                writer["ql"] = ("arrc%d" % r, count["arrc%d" % r])
+                for b in range(4):
+                    unpack(b, 4 + b, ql, sl, "ql")
+
+        def plane(b):
+            act(T.tp[:, C * b:C * b + C], T.ti[:, b:1024:4], F.Copy, ["ti%d" % b], ["tp%d" % b])
+
+        if r == 0:
+            late_constants()
+        plane(0)
+        plane(1)
+
+        for h in range(2):
+            tt(T.sums[:, halves[h]], bl[:].indirect(off(LB + 8 * h, 8)), T.apre[:, halves[h]], A.add, ["bl", "lb", "apre"], ["sums%d" % h])
+        for h in range(2):
+            tp(T.yy[:, halves[h]], T.sums[:, halves[h]], ["sums%d" % h], ["yy%d" % h])
+        for h in range(2):
+            scan(T.run[:, halves[h]], T.d0x[:, halves[h]], T.yy[:, halves[h]], A.add, A.max, ["d0x", "yy%d" % h], ["run%d" % h])
+        requantise(0)
+        cp(T.in4[:], T.run[:].indirect(off(L4, 2)), ["run0", "run1", "l4"], ["in4"])
+        requantise(1)
         tp(T.uu[:], T.in4[:], ["in4"], ["uu"])
         act(T.in3[:], T.uu[:].indirect(off(L6, 16)), F.Copy, ["uu", "l6"], ["in3"])
         act(T.qy[:], T.uu[:].indirect(off(LQ, 1)), F.Copy, ["uu", "lq"], ["qy"])
-        tt(T.cm[:], T.in4[:].indirect(off(LB, 16)), T.run[:], A.is_gt, ["in4", "run", "lb"], ["cm"])
+        tt(T.cm[:], T.in4[:].indirect(off(LB, 16)), T.run[:], A.is_gt, ["in4", "run0", "run1", "lb"], ["cm"])
+        scan(T.mrun[:], T.d0m[:], T.cm[:], A.mult, A.add, ["d0m", "cm"], ["mrun"])
         tp(T.brep[:], T.in3[:], ["in3"], ["brep"])
 
-        jobs = [(t, 0, 16 * t + 16) for t in range(15, NLO + NV - 1, -1)] + [(t, 16 * t + 16, C) for t in range(NLO)]
+        jobs = [(t, 0, 16 * t + 16) for t in range(15, NH - 1, -1)] + [(t, 16 * t + 16, C) for t in range(NLO)]
 
         def pass1(n):
             t, a, b = jobs[n]
@@ -272,47 +287,70 @@ def rank_program(g, core, T, topo):
             else:
                 act(w, w, F.Relu, ["sg%d" % t, "accz"], ["sg%d" % t, "acc%d" % t], scale=-1.0, accum_out=T.acc[:, t:t + 1])
 
-        pass1(0)
         for n in range(len(jobs)):
-            if n + 1 < len(jobs):
-                pass1(n + 1)
+            pass1(n)
+        before("s", ["sg%d" % jobs[-3][0]], [])
+        for n in range(len(jobs)):
+            if n == len(jobs) - 2:
+                before("s", ["sg%d" % jobs[-1][0]], [])
             pass2(n)
+        plane(2)
+        plane(3)
         for b in range(4):
             act(T.tb[:, C * b:C * b + C], bank(4 + b, C), F.Copy, ["ps%d" % (4 + b)], ["tb%d" % b], scale=0.5)
 
-        comps = []
-        for t in range(16):
-            o = sum(WID[:t]) + 2
-            if t < NLO + NV:
-                comps.append((o, 0, 16 * t + 16, t, A.is_ge))
-                o += 16 * t + 16
-            if NLO <= t < 15:
-                comps.append((o, 16 * t + 16, C, t, A.is_gt))
-        ckeys = []
+        def whole(t, side):
+            a, b, c = (0, 16 * t + 16, A.is_ge) if side == 0 else (16 * t + 16, C, A.is_gt)
+            o = C * (t - NLO)
+            ts(T.cmf[:, o + a:o + b], T.brep[:, a:b], T.qy[:, t:t + 1], None, c, None, ["brep", "qy"], ["f%d_%d" % (t, side)])
 
-        def comp(k):
-            for i in range(k):
-                if comps:
-                    o, a, b, t, c = comps.pop()
-                    ckeys.append("c%d" % o)
-                    ts(T.cmp[:, o:o + b - a], T.brep[:, a:b], T.qy[:, t:t + 1], None, c, None, ["brep", "qy"], [ckeys[-1]])
+        def short(t):
+            a, b, c = (0, 16 * t + 16, A.is_ge) if t < NLO else (16 * t + 16, C, A.is_gt)
+            ts(T.cmp[:, POS[t] + 2:POS[t + 1]], T.brep[:, a:b], T.qy[:, t:t + 1], None, c, None, ["brep", "qy"], ["c%d" % t])
 
-        scan(T.mrun[:], T.d0m[:], T.cm[:], A.mult, A.add, ["d0m", "cm"], ["mrun"])
+        def total(t):
+            o = C * (t - NLO)
+            scan(T.cnt[:, POS[t]:POS[t + 1]], T.cmf[:, o:o + 128], T.cmf[:, o + 128:o + C], A.add, A.add,
+                 ["f%d_0" % t, "f%d_1" % t, "eqs"], ["cnt%d" % t], first=T.eqs[:, 16 * t + 15:16 * t + 16])
+
+        def totals(a, b):
+            c = slice(POS[a], POS[b])
+            scan(T.cnt[:, c], T.d0[:, c], T.cmp[:, c], A.mult, A.add, d0all + ["heads"] + ["c%d" % t for t in range(a, b)], ["cnt%d" % a])
+
+        tt(T.mab[:], T.mrun[:].indirect(off(L4, 2)), T.cab[:], A.add, ["mrun", "l4", "cona", "conb"], ["mab"])
+        for y in range(2):
+            dma("y", "lm", ["mab"], ["vrow"] if y == 0 else ["vrow1"], T.vrow[y:128:16, :], T.mab[:, 16 * y:16 * y + 16])
+        writer["vrow"] = writer["vrow1"]
+        readers["mab"] = [writer["vrow"]]
+        if r == 0:
+            wait("y", ("sntc0", count["sntc0"]))
+            dma("y", "lw", [], [], T.qw[:].bitcast(dt.uint8), T.wc[:])
+            dma("y", "lw", [], ["qw"], T.sw[:], T.ws[:])
+        if r == 1:
+            dma("y", "lv", [], ["vt"], T.vt[:], T.v[:])
         tt(T.eqb[:], T.qy[:].indirect(off(LB, 16)), T.brep[:], A.is_equal, ["qy", "lb", "brep"], ["eqb"])
-        cp(T.in4m[:], T.mrun[:].indirect(off(L4, 2)), ["mrun", "l4"], ["in4m"])
-        scan(T.eqs[:], T.d0e[:], T.eqb[:], A.mult, A.add, ["d0e", "eqb"], ["eqs"])
-        tp(T.um[:], T.in4m[:], ["in4m"], ["um"])
-        cp(T.cmp[:].indirect(off(LH, 1)), T.eqs[:, 15:C:16], ["eqs", "lh", "cmpz"], ["heads"])
-        tt(T.inv[:, 0:C:16], T.um[:].indirect(off(LV, 1)), T.cona[:], A.add, ["um", "lv", "cona", "invz"], ["inva"])
-        ts(T.inv[:, 1:C:16], T.um[:].indirect(off(LV, 1)), pf(20), None, A.add, None, ["um", "lv", "conb", "invz"], ["invb"])
+        whole(NLO, 0)
+        whole(NLO, 1)
+        scan(T.eqs[:], T.d0e[:], T.eqb[:], A.mult, A.subtract, ["d0e", "eqb"], ["eqs"])
+        whole(NLO + 1, 0)
+        whole(NLO + 1, 1)
+        cp(T.cmp[:].indirect(off(LH, 1)), T.eqs[:, 15:C:16], ["eqs", "lh", "cmpz"] + ["c%d" % t for t in range(16)], ["heads"])
+        for t in range(NLO + 2, NH):
+            whole(t, 0)
+            whole(t, 1)
         before("v", ["heads"], [])
-        comp(1)
-        tp(T.vrow[:], T.inv[:], ["inva", "invb", "invz"], ["vrow"])
-        comp(99)
-        scan(T.cnt[:], T.d0[:], T.cmp[:], A.mult, A.add, d0all + ckeys + ["heads"], ["cnt"])
-        tt(T.rho[:], T.cnt[:].indirect(off(LE, 1)), T.acc[:], A.add, ["cnt", "le", "accz"] + ["acc%d" % j[0] for j in jobs], ["rho"])
+        for t in list(range(NLO)) + list(range(NH, 15)):
+            short(t)
+        before("v", ["f%d_1" % (NH - 1)], [])
+        for t in range(NLO, NH):
+            total(t)
+        before("v", ["c14"], [])
+        totals(0, NLO)
+        totals(NH, 16)
+        tt(T.rho[:], T.cnt[:].indirect(off(LE, 1)), T.acc[:], A.add,
+           ["cnt%d" % t for t in range(16)] + ["le", "accz"] + ["acc%d" % j[0] for j in jobs], ["rho"])
         ts(T.offr[:], T.rho[:], 16.0, None, A.add, None, ["rho"], ["offr"])
-        cp(T.ew[:].indirect(T.offr[:]), T.vrow[:], ["offr", "vrow", "ewz"], ["ew"])
+        cp(T.ew[:].indirect(T.offr[:]), T.vrow[:], ["offr", "vrow", "vrow1", "ewz"], ["ew"])
         tp(T.tr[:, 0:160], T.ew[:, 16:176], ["ew"], ["tr0"])
         tp(T.tr[:, 160:352], T.ew[:, 0:192], ["ew"], ["tr1"])
         cp(T.offab[:], T.tr[:].indirect(off(LX, 2)), ["tr0", "tr1", "lx"], ["offab"])
@@ -333,24 +371,28 @@ def rank_program(g, core, T, topo):
         for b in range(4):
             mm(4 + b, K, T.qw[:, 128 * b:128 * b + 128], T.sw[:, 128 * b:128 * b + 128], T.qz[:], T.sz[:], ["qw", "qz"])
             act(T.hs[:, HW * b + 16:HW * b + 16 + K], bank(4 + b, K), F.Copy, ["ps%d" % (4 + b)], ["hs%d" % b], scale=0.03125)
-            if b < 3:
-                tt(T.xs[:, b:1024:4], T.hs[:, HW * b:HW * b + HW].indirect(T.offr[:]), T.tp[:, C * b:C * b + C], A.add,
-                   ["hs%d" % b, "offr", "tp%d" % b] + hz, ["xs%d" % b])
         act(T.g3[:], T.hs[:, HW * 3:HW * 4].indirect(T.offr[:]), F.Copy, ["hs3", "offr"] + hz, ["g3"])
-        tt(T.xs[:, 3:1024:4], T.g3[:], bank(3, C), A.add, ["g3", "ps3"], ["xs3"])
-        xt, x_keys = T.xs, [["xs%d" % b for b in range(4)]] * 2
+        for b in range(3):
+            tt(T.xs[:, b:1024:4], T.hs[:, HW * b:HW * b + HW].indirect(T.offr[:]), T.tp[:, C * b:C * b + C], A.add,
+               ["hs%d" % b, "offr", "tp%d" % b] + hz, ["xs%d" % b])
+        for h in range(2):
+            tt(T.xs[:, 512 * h + 3:512 * h + 512:4], T.g3[:, halves[h]], T.ps[:, 1536 + 128 * h:1664 + 128 * h], A.add, ["g3", "ps3"], ["xs3%d" % h])
+        xt, x_keys = T.xs, [["xs0", "xs1", "xs2", "xs3%d" % h] for h in range(2)]
 
+    for s in SEMAPHORES:
+        if s.startswith("snt"):
+            wait("y", (s, count[s]))
     for h in range(2):
-        c = slice(128 * h, 128 * h + 128)
+        c = halves[h]
         qz(T.qx3[:, c], T.sx3[:, c], xt[:, 512 * h:512 * h + 512], x_keys[h], ["qx3%d" % h])
         mm(4 + h, 128, T.qv[:], T.sv[:], T.qx3[:, c], T.sx3[:, c], ["qv", "qx3%d" % h])
     writer["qx3"] = writer["qx31"]
     dma("y", "out", ["qx3"], [], T.oc[:], T.qx3[:].bitcast(dt.uint8))
     for k in range(4):
-        dma("y", "out", ["qx3"], [], T.osc[4 * k:4 * k + 4, :], T.sx3[32 * k:32 * k + 4, :])
-    act(T.yo[:, 0:128], bank(4, 128), F.Copy, ["ps4"], ["yo0"])
+        dma("ys"[k % 2], "out", ["qx3"], [], T.osc[4 * k:4 * k + 4, :], T.sx3[32 * k:32 * k + 4, :])
+    cp(T.yo[:, 0:128], bank(4, 128), ["ps4"], ["yo0"])
     cp(T.yo[:, 128:256], bank(5, 128), ["ps5"], ["yo1"])
     dma("s", "out", ["yo0", "yo1"], [], T.y[:], T.yo[:])
     for s in SEMAPHORES:
-        if count[s]:
+        if all(seen[q].get(s, 0) < count[s] for q in Q):
             wait("y", (s, count[s]))

@@ -1,31 +1,29 @@
-from concourse.mybir import dt, AluOpType, AxisListType, ActivationFunctionType
+from concourse.mybir import dt, AluOpType, ActivationFunctionType
 
 A = AluOpType
 F = ActivationFunctionType
 MASKS = [4, 1, 2]
 C, K = 256, 160
-NLO, NV = 4, 8
-NH = NLO + NV
-WID = [2 + 16 * t + 16 if t < NLO else C // 2 if t < NH else 2 + C - 16 * t - 16 for t in range(16)]
-POS = [sum(WID[:t]) for t in range(17)]
-CW = POS[16]
+SH, NH = 3, 13
+NV = NH - SH
+SW = C + 1
 HW = 272
 X4, BF, F32 = "float8_e4m3fn_x4", "bfloat16", "float32"
 SCRATCH = {"ps": ("psum", [128, 4096], F32)}
 for _d, _l in (
     (BF, dict(x0=1024, xs=1024, ut=512, vt=512, ones=516, eye=516, ti=1024, tp=1024, tb=1024, ah=4 * K, zt=4 * K, eqb=C, eqs=C,
-              cm=C, mrun=C, mab=32, vrow=C, ew=HW, tr=352, cmp=CW, cmf=C * NV, cnt=CW, d0=CW, sg=16 * C, zn=16, d0e=C, d0m=C)),
-    (F32, dict(hs=4 * HW + 16, ssb=288, stw=544, apre=C, sums=C, yy=C, run=C, in4=32, uu=32, in3=C, brep=C, qy=16, acc=16, rho=16,
-               wm=64, pf=24, i256=C, sq=C, g3=C, d0x=C, cab=32, yo=C, bs0=16, bs1=16, bs2=16, bl0=16, bl1=16, bl2=16)),
+              cm=C, mrun=C, mab=32, vrow=C, ew=HW, tr=352, cmf=C * NV, cnt=128 * NV, sg=16 * SW, zn=16, d0e=C, d0m=C)),
+    (F32, dict(hs=4 * HW + 16, ssb=288, stw=544, apre=128, sums=C, yy=C, run=C, in4=32, uu=32, in3=C, brep=C, qy=16, acc=32,
+               pf=24, i256=C, sq=C, g3=C, d0x=C, cab=32, yo=C, bs0=16, bs1=16, bs2=16, bl0=16, bl1=16, bl2=16)),
     (X4, dict(qu=128, qv=128, qw=512, qe=512, qz=K, qx0=C, qx1=C, qx2=C, qx3=C, qt0=C, qt1=C, qt2=C, ql0=C, ql1=C, ql2=C)),
     ("uint8", dict(su=128, sv=128, sw=512, se=512, sz=K, sx0=C, sx1=C, sx2=C, sx3=C, st0=C, st1=C, st2=C, sl0=C, sl1=C, sl2=C)),
-    ("uint16", dict(offr=16, offab=32, offc=80)), ("int32", dict(ic=112, pi=8)),
+    ("uint16", dict(offr=16, offab=32, offc=72)), ("int32", dict(ic=56, pi=8)),
 ):
     for _n in _l:
         SCRATCH[_n] = ("sbuf", [128, _l[_n]], _d)
 SEMAPHORES = ["nv", "ns", "nt", "ng", "lx", "lx1", "lu", "lv", "lw", "lm", "out"] + [
     "%s%d" % (n, r) for r in range(3) for n in ("arrs", "arrc", "snts", "sntc")]
-LB, L6, LAP, L4, LX, LQ, LH, LE, LN = 0, 32, 48, 64, 66, 68, 72, 74, 76
+LB, L6, LAP, L4, LX, LQ = 0, 32, 48, 64, 66, 68
 
 
 def rank_program(g, core, T, topo):
@@ -37,7 +35,6 @@ def rank_program(g, core, T, topo):
     count = {n: 0 for n in SEMAPHORES}
     seen = {q: {} for q in Q}
     writer, readers = {}, {}
-
     known = {}
 
     def wait(q, ev):
@@ -132,6 +129,12 @@ def rank_program(g, core, T, topo):
     def pf(i, n=1):
         return T.pf[:, i:i + n]
 
+    def zeros(key, buf, a, b):
+        act(buf[:, a:b], T.ones[:, 0:b - a], F.Identity, ["ones"], [key], scale=0.0)
+
+    def units(b):
+        qz(T.qe[:, 128 * b:128 * b + 128], T.se[:, 128 * b:128 * b + 128], T.eye[:, 3 - b:515 - b], ["eye"], ["qe%d" % b])
+
     dma("y", "lx", [], ["x00"], T.x0[:, 0:512], T.x[:, 0:512])
     dma("s", "lu", [], ["ut"], T.ut[:], T.u[:])
     dma("y", "lx1", [], ["x01"], T.x0[:, 512:1024], T.x[:, 512:1024])
@@ -139,45 +142,36 @@ def rank_program(g, core, T, topo):
     iota(T.pi[:, 0:1], [[1, 1]], 0, 1, ["p"])
     iota(T.ic[:, 0:16], [[1, 16]], 0, 0, ["ic0"])
     op("g", ["ones"], ["eye"], lambda: g.affine_select(T.eye[:], T.ones[:], [[-1, 516]], A.is_equal, 0.0, 3, 4))
-    iota(T.ic[:, 48:64], [[0, 8], [16, 2]], 0, 0, ["ic3"])
-    iota(T.ic[:, 32:48], [[2, 8], [16, 2]], 0, 0, ["ic2"])
-    iota(T.ic[:, 80:82], [[0, 2]], 15, 16, ["ic5"])
+    iota(T.ic[:, 16:24], [[0, 4], [16, 2]], 0, 0, ["ic1"])
     op("g", [], ["i256"], lambda: g.iota(T.i256[:], [[0, 16], [1, 16]], 0, 0, allow_small_or_imprecise_dtypes=True))
-    iota(T.ic[:, 96:96 + NLO], [[16, NLO]], WID[0], 0, ["w0"])
-    iota(T.ic[:, 96 + NLO:96 + NH], [[0, NV]], WID[NLO], 0, ["w1"])
-    iota(T.ic[:, 96 + NH:112], [[-16, 16 - NH]], WID[NH], 0, ["w2"])
-    for a in range(0, CW, 512):
-        b = min(a + 512, CW)
-        act(T.d0[:, a:b], T.ones[:, 0:b - a], F.Copy, ["ones"], ["d0_%d" % a])
-    d0keys = ["d0_%d" % a for a in range(0, CW, 512)]
+    iota(T.ic[:, 32:48], [[2, 8], [16, 2]], 0, 0, ["ic2"])
+    iota(T.ic[:, 48:50], [[0, 2]], 15, 16, ["ic3"])
+    zeros("vrow", T.vrow, 0, C)
+    zeros("ewz", T.ew, 0, 16)
+    zeros("ssbe", T.ssb, 0, 16)
+    zeros("ssbe2", T.ssb, 272, 288)
+    zeros("hq", T.hs, 0, 16)
+    for b in range(4):
+        zeros("hz%d" % b, T.hs, HW * b + 16 + K, HW * b + HW + 16)
     ts(T.pi[:, 1:2], T.pi[:, 0:1], 15, None, A.bitwise_and, None, ["p"], ["p1"])
     ts(T.pi[:, 2:3], T.pi[:, 0:1], 4, 1, A.logical_shift_right, A.bitwise_and, ["p"], ["p2"])
     ts(T.pi[:, 3:4], T.pi[:, 0:1], 1, None, A.bitwise_and, None, ["p"], ["p3"])
     ts(T.pi[:, 4:5], T.pi[:, 0:1], 31, None, A.bitwise_and, None, ["p"], ["p4"])
-    ms(T.ssb[:, 0:16], 0.0, ["ssbe"])
-    ms(T.ssb[:, 272:288], 0.0, ["ssbe2"])
-    cp(pf(0, 5), T.pi[:, 0:5], ["p", "p1", "p2", "p3", "p4"], ["pf"])
-    R, H, R0 = pf(1), pf(2), pf(3)
     ms(T.zn[:], 0.0, ["zn0"])
+    cp(off(LB, 16), T.ic[:, 0:16], ["ic0"], ["lb"])
+    cp(pf(0, 4), T.pi[:, 0:4], ["p", "p1", "p2", "p3"], ["pf"])
+    R, H, R0 = pf(1), pf(2), pf(3)
+    cp(off(LQ, 1), T.pi[:, 4:5], ["p4"], ["lq"])
+    ts(T.cab[:, 16:32], T.ic[:, 0:16], 16.0, None, A.mult, None, ["ic0"], ["conb"])
     tt(pf(6), R0, H, A.not_equal, ["pf"], ["par"])
     ts(pf(7), R, H, 16.0, A.subtract, A.mult, ["pf"], ["pf7"])
-    ms(T.vrow[:], 0.0, ["vrow"])
-    ts(pf(8), pf(6), 272.0, pf(7), A.mult, A.add, ["par", "pf7"], ["pf8"])
-    ms(T.acc[:], 0.0, ["accz"])
-    ms(T.ew[:, 0:16], 0.0, ["ewz"])
-    ms(T.hs[:, 0:16], 0.0, ["hq"])
-    cp(off(LQ, 1), T.pi[:, 4:5], ["p4"], ["lq"])
     ts(pf(10), R, 9.0, 16.0, A.min, A.mult, ["pf"], ["pf10"])
     ts(pf(20), R, 16.0, None, A.mult, None, ["pf"], ["pf20"])
-    cp(off(LB, 16), T.ic[:, 0:16], ["ic0"], ["lb"])
-    ts(T.wm[:, 0:16], T.ic[:, 0:16], R, None, A.is_lt, None, ["ic0", "pf"], ["wm0"])
+    ts(pf(8), pf(6), 272.0, pf(7), A.mult, A.add, ["par", "pf7"], ["pf8"])
     ts(pf(11), pf(6), 176.0, pf(10), A.mult, A.add, ["par", "pf10"], ["pf11"])
-    ts(T.wm[:, 16:32], T.ic[:, 0:16], R, None, A.is_le, None, ["ic0", "pf"], ["wm1"])
     ts(T.cab[:, 0:16], T.zn[:], pf(20), None, A.add, None, ["zn0", "pf20"], ["cona"])
-    ts(T.cab[:, 16:32], T.ic[:, 0:16], 16.0, None, A.mult, None, ["ic0"], ["conb"])
     ts(off(LX, 2), T.ic[:, 0:2], pf(11), None, A.add, None, ["ic0", "pf11"], ["lx"])
-    for b in range(4):
-        qz(T.qe[:, 128 * b:128 * b + 128], T.se[:, 128 * b:128 * b + 128], T.eye[:, 3 - b:515 - b], ["eye"], ["qe%d" % b])
+    units(2)
     act(T.d0m[:], T.i256[:], F.Sign, ["i256"], ["d0m"])
     act(T.sq[:], T.i256[:], F.Square, ["i256", "pf"], ["sq"], bias=R, scale=-1.0)
     act(T.d0x[:], T.d0m[:], F.Relu, ["d0m"], ["d0y"], bias=1.0, scale=-1.0)
@@ -186,20 +180,10 @@ def rank_program(g, core, T, topo):
     def late_constants():
         act(T.d0x[:], T.d0x[:], F.Copy, ["d0y"], ["d0x"], scale=-1.0e29)
         act(T.d0e[:], T.sq[:], F.Sign, ["sq"], ["d0e"])
-        tt(T.wm[:, 32:48], T.wm[:, 0:16], T.ic[:, 96:112], A.mult, ["wm0", "w0", "w1", "w2"], ["wm2"])
-        tt(T.wm[:, 48:64], T.wm[:, 16:32], T.ic[:, 96:112], A.mult, ["wm1", "w0", "w1", "w2"], ["wm3"])
-        ts(T.ic[:, 82:84], T.ic[:, 80:82], 255, None, A.bitwise_and, None, ["ic5"], ["ic6"])
-        op("v", ["wm2"], ["pf16"], lambda: V.tensor_reduce(pf(16), T.wm[:, 32:48], AxisListType.X, A.add))
-        op("v", ["wm3"], ["pf17"], lambda: V.tensor_reduce(pf(17), T.wm[:, 48:64], AxisListType.X, A.add))
+        ts(T.ic[:, 50:52], T.ic[:, 48:50], 255, None, A.bitwise_and, None, ["ic3"], ["ic4"])
         ts(off(L6, 16), T.ic[:, 32:48], H, None, A.add, None, ["ic2", "pf"], ["l6"])
-        cp(off(L4, 2), T.ic[:, 82:84], ["ic6"], ["l4"])
-        cp(off(LH, 1), pf(16), ["pf16"], ["lh"])
-        ts(off(LN, 1), pf(16), 1.0, None, A.add, None, ["pf16"], ["ln"])
-        ts(off(LE, 1), pf(17), -1.0, None, A.add, None, ["pf17"], ["le"])
-        cp(T.d0[:].indirect(off(LH, 1)), T.zn[:], d0keys + ["lh", "zn0"], ["d0h"])
-        cp(T.cmp[:].indirect(off(LN, 1)), T.zn[:], ["ln", "zn0"], ["cmpz"])
+        cp(off(L4, 2), T.ic[:, 50:52], ["ic4"], ["l4"])
 
-    d0all = d0keys + ["d0h"]
     hz = ["hq", "hz0", "hz1", "hz2", "hz3"]
     halves = [slice(0, 128), slice(128, C)]
     xt, x_keys = T.x0, [["x00"], ["x01"]]
@@ -221,22 +205,23 @@ def rank_program(g, core, T, topo):
             qz(qx[:, c], sx[:, c], xt[:, 512 * h:512 * h + 512], x_keys[h], ["qx%d%d" % (r, h)])
             mm(6 + h, 128, T.qu[:], T.su[:], qx[:, c], sx[:, c], ["qu", "qx%d%d" % (r, h)])
         writer["qx%d" % r] = writer["qx%d1" % r]
-        for b in (2, 0, 1, 3):
-            unpack(b, b, qx, sx, "qx%d" % r)
         for h in range(2):
             tp(T.stw[:, halves[h]], bank(6 + h, 128), ["ps%d" % (6 + h)], ["stw%d" % h])
         cp(bs[:], T.stw[:, 1:256:16], ["stw0", "stw1"], ["bs%d" % r])
         send(bl[:], bs[:], eng, "arrs%d" % r, "snts%d" % r, ["bs%d" % r])
         writer["bl"] = ("arrs%d" % r, count["arrs%d" % r])
         if r == 0:
-            ts(off(LAP, 16), T.ic[:, 48:64], pf(8), None, A.add, None, ["ic3", "pf8"], ["lap"])
+            ts(off(LAP, 8), T.ic[:, 16:24], pf(8), None, A.add, None, ["ic1", "pf8"], ["lap"])
+            for b in (0, 1, 3):
+                units(b)
+        for b in (2, 0, 1, 3):
+            unpack(b, b, qx, sx, "qx%d" % r)
         for h in range(2):
             act(T.ssb[:, 16 + 128 * h:144 + 128 * h], bank(6 + h, 128), F.Copy, ["ps%d" % (6 + h)], ["ssb%d" % h])
         tp(T.stw[:, 256:544], T.ssb[:], ["ssb0", "ssb1", "ssbe", "ssbe2"], ["stw2"])
-        act(T.apre[:], T.stw[:].indirect(off(LAP, 16)), F.Copy, ["stw0", "stw1", "stw2", "lap"], ["apre"])
-        for b in (2, 0):
-            cp(T.ti[:, b:1024:4], bank(b, C), ["ps%d" % b], ["ti%d" % b])
-        for b in (1, 3):
+        act(T.apre[:], T.stw[:].indirect(off(LAP, 8)), F.Copy, ["stw0", "stw1", "stw2", "lap"], ["apre"])
+        cp(T.ti[:, 2:1024:4], bank(2, C), ["ps2"], ["ti2"])
+        for b in (0, 1, 3):
             act(T.ti[:, b:1024:4], bank(b, C), F.Copy, ["ps%d" % b], ["ti%d" % b])
 
         def requantise(h):
@@ -258,7 +243,7 @@ def rank_program(g, core, T, topo):
         plane(1)
 
         for h in range(2):
-            tt(T.sums[:, halves[h]], bl[:].indirect(off(LB + 8 * h, 8)), T.apre[:, halves[h]], A.add, ["bl", "lb", "apre"], ["sums%d" % h])
+            tt(T.sums[:, halves[h]], bl[:].indirect(off(LB + 8 * h, 8)), T.apre[:], A.add, ["bl", "lb", "apre"], ["sums%d" % h])
         for h in range(2):
             tp(T.yy[:, halves[h]], T.sums[:, halves[h]], ["sums%d" % h], ["yy%d" % h])
         for h in range(2):
@@ -267,55 +252,58 @@ def rank_program(g, core, T, topo):
         cp(T.in4[:], T.run[:].indirect(off(L4, 2)), ["run0", "run1", "l4"], ["in4"])
         requantise(1)
         tp(T.uu[:], T.in4[:], ["in4"], ["uu"])
-        act(T.in3[:], T.uu[:].indirect(off(L6, 16)), F.Copy, ["uu", "l6"], ["in3"])
+        for h in range(2):
+            act(T.in3[:, halves[h]], T.uu[:].indirect(off(L6 + 8 * h, 8)), F.Copy, ["uu", "l6"], ["in3%d" % h])
         act(T.qy[:], T.uu[:].indirect(off(LQ, 1)), F.Copy, ["uu", "lq"], ["qy"])
         tt(T.cm[:], T.in4[:].indirect(off(LB, 16)), T.run[:], A.is_gt, ["in4", "run0", "run1", "lb"], ["cm"])
+        tp(T.brep[:, halves[0]], T.in3[:, halves[0]], ["in30"], ["brep0"])
         scan(T.mrun[:], T.d0m[:], T.cm[:], A.mult, A.add, ["d0m", "cm"], ["mrun"])
-        tp(T.brep[:], T.in3[:], ["in3"], ["brep"])
+        tp(T.brep[:, halves[1]], T.in3[:, halves[1]], ["in31"], ["brep"])
 
-        jobs = [(t, 0, 16 * t + 16) for t in range(15, NH - 1, -1)] + [(t, 16 * t + 16, C) for t in range(NLO)]
+        low, high = list(range(SH)), list(range(15, NH - 1, -1))
 
-        def pass1(n):
-            t, a, b = jobs[n]
-            act(T.sg[:, C * t:C * t + b - a], T.brep[:, a:b], F.Sign, ["brep", "qy"], ["sg%d" % t], bias=T.qy[:, t:t + 1], scale=-1.0)
+        def signs(t, a, b):
+            act(T.sg[:, SW * t + a:SW * t + b], T.brep[:, a:b], F.Sign, ["brep0" if b <= 128 else "brep", "qy"],
+                ["sg%d" % t, "sa%d" % t, "sb%d" % t], bias=T.qy[:, t:t + 1], scale=-1.0)
 
-        def pass2(n):
-            t, a, b = jobs[n]
-            w = T.sg[:, C * t:C * t + b - a]
-            if a == 0:
-                act(w, w, F.Sign, ["sg%d" % t, "accz"], ["sg%d" % t, "acc%d" % t], bias=1.0, scale=-1.0, accum_out=T.acc[:, t:t + 1])
-            else:
-                act(w, w, F.Relu, ["sg%d" % t, "accz"], ["sg%d" % t, "acc%d" % t], scale=-1.0, accum_out=T.acc[:, t:t + 1])
+        def left(t):
+            w = T.sg[:, SW * t:SW * t + 16 * t + 16]
+            act(w, w, F.Sign, ["sg%d" % t], ["sa%d" % t], bias=1.0, scale=-1.0, accum_out=T.acc[:, t:t + 1])
 
-        for n in range(len(jobs)):
-            pass1(n)
-        before("s", ["sg%d" % jobs[-3][0]], [])
-        for n in range(len(jobs)):
-            if n == len(jobs) - 2:
-                before("s", ["sg%d" % jobs[-1][0]], [])
-            pass2(n)
-        plane(2)
-        plane(3)
-        for b in range(4):
-            act(T.tb[:, C * b:C * b + C], bank(4 + b, C), F.Copy, ["ps%d" % (4 + b)], ["tb%d" % b], scale=0.5)
+        def right(t):
+            w = T.sg[:, SW * t + 16 * t + 15:SW * t + C] if t == SH else T.sg[:, SW * t + 16 * t + 16:SW * t + SW]
+            act(w, w, F.Relu, ["sg%d" % t, "slot%d" % t], ["sb%d" % t], scale=-1.0, accum_out=T.acc[:, 16 + t:17 + t])
 
-        def whole(t, side):
-            a, b, c = (0, 16 * t + 16, A.is_ge) if side == 0 else (16 * t + 16, C, A.is_gt)
-            o = C * (t - NLO)
-            ts(T.cmf[:, o + a:o + b], T.brep[:, a:b], T.qy[:, t:t + 1], None, c, None, ["brep", "qy"], ["f%d_%d" % (t, side)])
-
-        def short(t):
-            a, b, c = (0, 16 * t + 16, A.is_ge) if t < NLO else (16 * t + 16, C, A.is_gt)
-            ts(T.cmp[:, POS[t] + 2:POS[t + 1]], T.brep[:, a:b], T.qy[:, t:t + 1], None, c, None, ["brep", "qy"], ["c%d" % t])
+        def whole(t, sides=(0, 1)):
+            for side in sides:
+                a, b, c = (0, 16 * t + 16, A.is_ge) if side == 0 else (16 * t + 16, C, A.is_gt)
+                o = C * (t - SH)
+                ts(T.cmf[:, o + a:o + b], T.brep[:, a:b], T.qy[:, t:t + 1], -1.0, c, A.mult, ["brep", "qy"], ["f%d_%d" % (t, side)])
 
         def total(t):
-            o = C * (t - NLO)
-            scan(T.cnt[:, POS[t]:POS[t + 1]], T.cmf[:, o:o + 128], T.cmf[:, o + 128:o + C], A.add, A.add,
-                 ["f%d_0" % t, "f%d_1" % t, "eqs"], ["cnt%d" % t], first=T.eqs[:, 16 * t + 15:16 * t + 16])
+            o, w = C * (t - SH), 8 * t + 8 if t == SH else 128
+            out = T.sg[:, SW * t + w:SW * t + 2 * w] if t == SH else T.cnt[:, 128 * (t - SH):128 * (t - SH) + 128]
+            scan(out, T.cmf[:, o:o + w], T.cmf[:, o + w:o + 2 * w], A.add, A.add, ["f%d_0" % t, "f%d_1" % t, "eqs"],
+                 ["slot%d" % t], first=T.eqs[:, 16 * t + 15:16 * t + 16])
 
-        def totals(a, b):
-            c = slice(POS[a], POS[b])
-            scan(T.cnt[:, c], T.d0[:, c], T.cmp[:, c], A.mult, A.add, d0all + ["heads"] + ["c%d" % t for t in range(a, b)], ["cnt%d" % a])
+        def slots(a, b):
+            tt(T.sg[:, SW * a + C:SW * b:SW], T.eqs[:, 16 * a + 15:16 * b:16], T.acc[:, a:b], A.subtract,
+               ["eqs"] + ["sa%d" % t for t in range(a, b)], ["slot%d" % t for t in range(a, b)])
+
+        def places(a, b):
+            ts(T.offr[:, a:b], T.acc[:, 16 + a:16 + b], 16.0, None, A.add, None, ["sb%d" % t for t in range(a, b)], ["offr%d" % a])
+
+        for t in high[:2]:
+            signs(t, 0, 128)
+        for t in low + high[2:]:
+            signs(t, 0, C)
+        for t in low:
+            left(t)
+        for t in high[:2]:
+            signs(t, 128, C)
+        signs(SH, 16 * SH + 16, C)
+        for t in high[2:] + high[:2]:
+            left(t)
 
         tt(T.mab[:], T.mrun[:].indirect(off(L4, 2)), T.cab[:], A.add, ["mrun", "l4", "cona", "conb"], ["mab"])
         for y in range(2):
@@ -329,28 +317,31 @@ def rank_program(g, core, T, topo):
         if r == 1:
             dma("y", "lv", [], ["vt"], T.vt[:], T.v[:])
         tt(T.eqb[:], T.qy[:].indirect(off(LB, 16)), T.brep[:], A.is_equal, ["qy", "lb", "brep"], ["eqb"])
-        whole(NLO, 0)
-        whole(NLO, 1)
-        scan(T.eqs[:], T.d0e[:], T.eqb[:], A.mult, A.subtract, ["d0e", "eqb"], ["eqs"])
-        whole(NLO + 1, 0)
-        whole(NLO + 1, 1)
-        cp(T.cmp[:].indirect(off(LH, 1)), T.eqs[:, 15:C:16], ["eqs", "lh", "cmpz"] + ["c%d" % t for t in range(16)], ["heads"])
-        for t in range(NLO + 2, NH):
-            whole(t, 0)
-            whole(t, 1)
-        before("v", ["heads"], [])
-        for t in list(range(NLO)) + list(range(NH, 15)):
-            short(t)
-        before("v", ["f%d_1" % (NH - 1)], [])
-        for t in range(NLO, NH):
+        whole(SH + 1)
+        scan(T.eqs[:], T.d0e[:], T.eqb[:], A.mult, A.add, ["d0e", "eqb"], ["eqs"])
+        whole(SH, (0,))
+        for t in range(SH + 2, NH):
+            whole(t)
+            if t == NH - 4:
+                slots(0, SH)
+                total(SH)
+        for t in low + [SH]:
+            right(t)
+        for t in range(SH + 1, NH):
+            if t == SH + 3:
+                slots(NH, 16)
             total(t)
-        before("v", ["c14"], [])
-        totals(0, NLO)
-        totals(NH, 16)
-        tt(T.rho[:], T.cnt[:].indirect(off(LE, 1)), T.acc[:], A.add,
-           ["cnt%d" % t for t in range(16)] + ["le", "accz"] + ["acc%d" % j[0] for j in jobs], ["rho"])
-        ts(T.offr[:], T.rho[:], 16.0, None, A.add, None, ["rho"], ["offr"])
-        cp(T.ew[:].indirect(T.offr[:]), T.vrow[:], ["offr", "vrow", "vrow1", "ewz"], ["ew"])
+        for t in high:
+            right(t)
+        plane(2)
+        plane(3)
+        for b in range(4):
+            act(T.tb[:, C * b:C * b + C], bank(4 + b, C), F.Copy, ["ps%d" % (4 + b)], ["tb%d" % b], scale=0.5)
+        places(0, SH + 1)
+        ts(T.offr[:, SH + 1:NH], T.cnt[:, 255:128 * NV:128], -1.0, 16.0, A.mult, A.add, ["slot%d" % t for t in range(SH + 1, NH)], ["offr"])
+        places(NH, 16)
+        offr = ["offr", "offr0", "offr%d" % NH]
+        cp(T.ew[:].indirect(T.offr[:]), T.vrow[:], offr + ["vrow", "vrow1", "ewz"], ["ew"])
         tp(T.tr[:, 0:160], T.ew[:, 16:176], ["ew"], ["tr0"])
         tp(T.tr[:, 160:352], T.ew[:, 0:192], ["ew"], ["tr1"])
         cp(T.offab[:], T.tr[:].indirect(off(LX, 2)), ["tr0", "tr1", "lx"], ["offab"])
@@ -359,9 +350,6 @@ def rank_program(g, core, T, topo):
         for b in (1, 2, 3):
             act(T.ah[:, K * b:K * b + K], T.tp[:, C * b:C * b + C].indirect(T.offab[:, 0:10]), F.Copy,
                 ["tp%d" % b, "offab"], ["ah%d" % b], scale=0.5)
-        if r == 0:
-            for b in range(4):
-                act(T.hs[:, HW * b + 16 + K:HW * b + HW + 16], T.ones[:, 0:HW - K], F.Identity, ["ones"], ["hz%d" % b], scale=0.0)
         for b in (1, 0, 2, 3):
             tt(T.zt[:, b:4 * K:4], T.tb[:, C * b:C * b + C].indirect(T.offab[:, 16:26]), T.ah[:, K * b:K * b + K], A.add,
                ["tb%d" % b, "ah%d" % b, "offab"], ["zt%d" % b])
@@ -371,10 +359,10 @@ def rank_program(g, core, T, topo):
         for b in range(4):
             mm(4 + b, K, T.qw[:, 128 * b:128 * b + 128], T.sw[:, 128 * b:128 * b + 128], T.qz[:], T.sz[:], ["qw", "qz"])
             act(T.hs[:, HW * b + 16:HW * b + 16 + K], bank(4 + b, K), F.Copy, ["ps%d" % (4 + b)], ["hs%d" % b], scale=0.03125)
-        act(T.g3[:], T.hs[:, HW * 3:HW * 4].indirect(T.offr[:]), F.Copy, ["hs3", "offr"] + hz, ["g3"])
+        act(T.g3[:], T.hs[:, HW * 3:HW * 4].indirect(T.offr[:]), F.Copy, ["hs3"] + offr + hz, ["g3"])
         for b in range(3):
             tt(T.xs[:, b:1024:4], T.hs[:, HW * b:HW * b + HW].indirect(T.offr[:]), T.tp[:, C * b:C * b + C], A.add,
-               ["hs%d" % b, "offr", "tp%d" % b] + hz, ["xs%d" % b])
+               ["hs%d" % b, "tp%d" % b] + offr + hz, ["xs%d" % b])
         for h in range(2):
             tt(T.xs[:, 512 * h + 3:512 * h + 512:4], T.g3[:, halves[h]], T.ps[:, 1536 + 128 * h:1664 + 128 * h], A.add, ["g3", "ps3"], ["xs3%d" % h])
         xt, x_keys = T.xs, [["xs0", "xs1", "xs2", "xs3%d" % h] for h in range(2)]

@@ -7,23 +7,23 @@ C, K = 256, 160
 SH, NH = 3, 13
 NV = NH - SH
 SW = C + 1
-HW = 272
+PW = C + K
 X4, BF, F32 = "float8_e4m3fn_x4", "bfloat16", "float32"
 SCRATCH = {"ps": ("psum", [128, 4096], F32)}
 for _d, _l in (
-    (BF, dict(x0=1024, xs=1024, ut=512, vt=512, ones=516, eye=516, ti=1024, tp=1024, tb=1024, ah=4 * K, zt=4 * K, eqb=C, eqs=C,
-              cm=C, mrun=C, mab=32, vrow=C, ew=HW, tr=352, cmf=C * NV, cnt=128 * NV, sg=16 * SW, zn=16, d0e=C, d0m=C)),
-    (F32, dict(hs=4 * HW + 16, ssb=288, stw=544, apre=128, sums=C, yy=C, run=C, in4=32, uu=32, in3=C, brep=C, qy=16, acc=32,
-               pf=24, i256=C, sq=C, g3=C, d0x=C, cab=32, yo=C, bs0=16, bs1=16, bs2=16, bl0=16, bl1=16, bl2=16)),
+    (BF, dict(x0=1024, xs=1024, ut=512, vt=512, ones=516, eye=516, ti=1024, tp=4 * PW, tb=1024, ah=4 * K, te=4 * K, zt=4 * K, eqb=C,
+              eqs=C, cm=C, mrun=C, mab=32, vrow=C, ew=288, tr=2 * K, cmf=C * NV, cnt=128 * NV, sg=16 * SW, zn=16, d0e=C, d0m=C)),
+    (F32, dict(sel=48, c16=16, ssb=288, stw=544, apre=128, sums=C, yy=C, run=C, in4=32, uu=32, in3=C, brep=C, qy=16, acc=32,
+               pf=24, i256=C, sq=C, d0x=C, cab=32, yo=C, bs0=16, bs1=16, bs2=16, bl0=16, bl1=16, bl2=16)),
     (X4, dict(qu=128, qv=128, qw=512, qe=512, qz=K, qx0=C, qx1=C, qx2=C, qx3=C, qt0=C, qt1=C, qt2=C, ql0=C, ql1=C, ql2=C)),
     ("uint8", dict(su=128, sv=128, sw=512, se=512, sz=K, sx0=C, sx1=C, sx2=C, sx3=C, st0=C, st1=C, st2=C, sl0=C, sl1=C, sl2=C)),
-    ("uint16", dict(offr=16, offab=32, offc=72)), ("int32", dict(ic=56, pi=8)),
+    ("uint16", dict(offr=16, offx=16, offab=48, offc=72)), ("int32", dict(ic=56, pi=8)),
 ):
     for _n in _l:
         SCRATCH[_n] = ("sbuf", [128, _l[_n]], _d)
 SEMAPHORES = ["nv", "ns", "nt", "ng", "lx", "lx1", "lu", "lv", "lw", "lm", "out"] + [
     "%s%d" % (n, r) for r in range(3) for n in ("arrs", "arrc", "snts", "sntc")]
-LB, L6, LAP, L4, LX, LQ = 0, 32, 48, 64, 66, 68
+LB, L6, LAP, L4, LX, LQ = 0, 32, 48, 64, 66, 70
 
 
 def rank_program(g, core, T, topo):
@@ -141,18 +141,14 @@ def rank_program(g, core, T, topo):
     ms(T.ones[:], 1.0, ["ones"])
     iota(T.pi[:, 0:1], [[1, 1]], 0, 1, ["p"])
     iota(T.ic[:, 0:16], [[1, 16]], 0, 0, ["ic0"])
+    op("g", [], ["i256"], lambda: g.iota(T.i256[:], [[0, 16], [1, 16]], 0, 0, allow_small_or_imprecise_dtypes=True))
     op("g", ["ones"], ["eye"], lambda: g.affine_select(T.eye[:], T.ones[:], [[-1, 516]], A.is_equal, 0.0, 3, 4))
     iota(T.ic[:, 16:24], [[0, 4], [16, 2]], 0, 0, ["ic1"])
-    op("g", [], ["i256"], lambda: g.iota(T.i256[:], [[0, 16], [1, 16]], 0, 0, allow_small_or_imprecise_dtypes=True))
     iota(T.ic[:, 32:48], [[2, 8], [16, 2]], 0, 0, ["ic2"])
     iota(T.ic[:, 48:50], [[0, 2]], 15, 16, ["ic3"])
-    zeros("vrow", T.vrow, 0, C)
-    zeros("ewz", T.ew, 0, 16)
+    zeros("ewz", T.ew, 16, 32)
     zeros("ssbe", T.ssb, 0, 16)
     zeros("ssbe2", T.ssb, 272, 288)
-    zeros("hq", T.hs, 0, 16)
-    for b in range(4):
-        zeros("hz%d" % b, T.hs, HW * b + 16 + K, HW * b + HW + 16)
     ts(T.pi[:, 1:2], T.pi[:, 0:1], 15, None, A.bitwise_and, None, ["p"], ["p1"])
     ts(T.pi[:, 2:3], T.pi[:, 0:1], 4, 1, A.logical_shift_right, A.bitwise_and, ["p"], ["p2"])
     ts(T.pi[:, 3:4], T.pi[:, 0:1], 1, None, A.bitwise_and, None, ["p"], ["p3"])
@@ -168,23 +164,20 @@ def rank_program(g, core, T, topo):
     ts(pf(10), R, 9.0, 16.0, A.min, A.mult, ["pf"], ["pf10"])
     ts(pf(20), R, 16.0, None, A.mult, None, ["pf"], ["pf20"])
     ts(pf(8), pf(6), 272.0, pf(7), A.mult, A.add, ["par", "pf7"], ["pf8"])
-    ts(pf(11), pf(6), 176.0, pf(10), A.mult, A.add, ["par", "pf10"], ["pf11"])
+    ts(pf(12), H, 16.0, 16.0, A.mult, A.add, ["pf"], ["pf12"])
+    ts(pf(11), R0, 144.0, pf(10), A.mult, A.add, ["pf", "pf10"], ["pf11"])
     ts(T.cab[:, 0:16], T.zn[:], pf(20), None, A.add, None, ["zn0", "pf20"], ["cona"])
-    ts(off(LX, 2), T.ic[:, 0:2], pf(11), None, A.add, None, ["ic0", "pf11"], ["lx"])
-    units(2)
     act(T.d0m[:], T.i256[:], F.Sign, ["i256"], ["d0m"])
     act(T.sq[:], T.i256[:], F.Square, ["i256", "pf"], ["sq"], bias=R, scale=-1.0)
-    act(T.d0x[:], T.d0m[:], F.Relu, ["d0m"], ["d0y"], bias=1.0, scale=-1.0)
+    act(T.d0x[:], T.d0m[:], F.Identity, ["d0m"], ["d0x"], bias=-1.0e29, scale=1.0e29)
+    act(T.d0e[:], T.sq[:], F.Sign, ["sq"], ["d0e"])
     qz(T.qu[:], T.su[:], T.ut[:], ["ut"], ["qu"])
 
     def late_constants():
-        act(T.d0x[:], T.d0x[:], F.Copy, ["d0y"], ["d0x"], scale=-1.0e29)
-        act(T.d0e[:], T.sq[:], F.Sign, ["sq"], ["d0e"])
         ts(T.ic[:, 50:52], T.ic[:, 48:50], 255, None, A.bitwise_and, None, ["ic3"], ["ic4"])
         ts(off(L6, 16), T.ic[:, 32:48], H, None, A.add, None, ["ic2", "pf"], ["l6"])
         cp(off(L4, 2), T.ic[:, 50:52], ["ic4"], ["l4"])
 
-    hz = ["hq", "hz0", "hz1", "hz2", "hz3"]
     halves = [slice(0, 128), slice(128, C)]
     xt, x_keys = T.x0, [["x00"], ["x01"]]
     for r in range(3):
@@ -205,20 +198,28 @@ def rank_program(g, core, T, topo):
             qz(qx[:, c], sx[:, c], xt[:, 512 * h:512 * h + 512], x_keys[h], ["qx%d%d" % (r, h)])
             mm(6 + h, 128, T.qu[:], T.su[:], qx[:, c], sx[:, c], ["qu", "qx%d%d" % (r, h)])
         writer["qx%d" % r] = writer["qx%d1" % r]
+        if r == 0:
+            ts(pf(13), pf(11), pf(12), -16.0, A.add, A.add, ["pf11", "pf12"], ["pf13"])
+            ts(T.c16[:], T.cab[:, 16:32], R, None, A.add, None, ["conb", "pf"], ["c16"])
         for h in range(2):
             tp(T.stw[:, halves[h]], bank(6 + h, 128), ["ps%d" % (6 + h)], ["stw%d" % h])
+        if r == 0:
+            cp(off(LX, 1), pf(13), ["pf13"], ["lx"])
+            ts(off(LX + 2, 2), T.ic[:, 1:3], pf(13), None, A.add, None, ["ic0", "pf13"], ["lx2"])
         cp(bs[:], T.stw[:, 1:256:16], ["stw0", "stw1"], ["bs%d" % r])
-        send(bl[:], bs[:], eng, "arrs%d" % r, "snts%d" % r, ["bs%d" % r])
+        send(bl[:], bs[:], eng[:8], "arrs%d" % r, "snts%d" % r, ["bs%d" % r])
         writer["bl"] = ("arrs%d" % r, count["arrs%d" % r])
         if r == 0:
+            op("g", [], ["vrow"], lambda: g.iota(T.vrow[:], [[1, C]], 0, 0, allow_small_or_imprecise_dtypes=True))
             ts(off(LAP, 8), T.ic[:, 16:24], pf(8), None, A.add, None, ["ic1", "pf8"], ["lap"])
-            for b in (0, 1, 3):
-                units(b)
-        for b in (2, 0, 1, 3):
-            unpack(b, b, qx, sx, "qx%d" % r)
+            units(2)
         for h in range(2):
             act(T.ssb[:, 16 + 128 * h:144 + 128 * h], bank(6 + h, 128), F.Copy, ["ps%d" % (6 + h)], ["ssb%d" % h])
         tp(T.stw[:, 256:544], T.ssb[:], ["ssb0", "ssb1", "ssbe", "ssbe2"], ["stw2"])
+        for b in (2, 0, 1, 3):
+            if r == 0 and b != 2:
+                units(b)
+            unpack(b, b, qx, sx, "qx%d" % r)
         act(T.apre[:], T.stw[:].indirect(off(LAP, 8)), F.Copy, ["stw0", "stw1", "stw2", "lap"], ["apre"])
         cp(T.ti[:, 2:1024:4], bank(2, C), ["ps2"], ["ti2"])
         for b in (0, 1, 3):
@@ -235,7 +236,7 @@ def rank_program(g, core, T, topo):
                     unpack(b, 4 + b, ql, sl, "ql")
 
         def plane(b):
-            act(T.tp[:, C * b:C * b + C], T.ti[:, b:1024:4], F.Copy, ["ti%d" % b], ["tp%d" % b])
+            act(T.tp[:, PW * b:PW * b + C], T.ti[:, b:1024:4], F.Copy, ["ti%d" % b], ["tp%d" % b], scale=32.0)
 
         if r == 0:
             late_constants()
@@ -249,13 +250,14 @@ def rank_program(g, core, T, topo):
         for h in range(2):
             scan(T.run[:, halves[h]], T.d0x[:, halves[h]], T.yy[:, halves[h]], A.add, A.max, ["d0x", "yy%d" % h], ["run%d" % h])
         requantise(0)
-        cp(T.in4[:], T.run[:].indirect(off(L4, 2)), ["run0", "run1", "l4"], ["in4"])
+        cp(T.in4[:, 0:16], T.run[:, 15:C:16], ["run0", "run1"], ["in4"])
+        act(T.in4[:, 16:32], T.run[:, 15:C:16], F.Copy, ["run0", "run1"], ["in4b"])
         requantise(1)
-        tp(T.uu[:], T.in4[:], ["in4"], ["uu"])
+        tp(T.uu[:], T.in4[:], ["in4", "in4b"], ["uu"])
         for h in range(2):
             act(T.in3[:, halves[h]], T.uu[:].indirect(off(L6 + 8 * h, 8)), F.Copy, ["uu", "l6"], ["in3%d" % h])
         act(T.qy[:], T.uu[:].indirect(off(LQ, 1)), F.Copy, ["uu", "lq"], ["qy"])
-        tt(T.cm[:], T.in4[:].indirect(off(LB, 16)), T.run[:], A.is_gt, ["in4", "run0", "run1", "lb"], ["cm"])
+        tt(T.cm[:], T.in4[:, 0:16].indirect(off(LB, 16)), T.run[:], A.is_gt, ["in4", "run0", "run1", "lb"], ["cm"])
         tp(T.brep[:, halves[0]], T.in3[:, halves[0]], ["in30"], ["brep0"])
         scan(T.mrun[:], T.d0m[:], T.cm[:], A.mult, A.add, ["d0m", "cm"], ["mrun"])
         tp(T.brep[:, halves[1]], T.in3[:, halves[1]], ["in31"], ["brep"])
@@ -291,7 +293,7 @@ def rank_program(g, core, T, topo):
                ["eqs"] + ["sa%d" % t for t in range(a, b)], ["slot%d" % t for t in range(a, b)])
 
         def places(a, b):
-            ts(T.offr[:, a:b], T.acc[:, 16 + a:16 + b], 16.0, None, A.add, None, ["sb%d" % t for t in range(a, b)], ["offr%d" % a])
+            ts(T.offr[:, a:b], T.acc[:, 16 + a:16 + b], pf(12), None, A.add, None, ["pf12"] + ["sb%d" % t for t in range(a, b)], ["offr%d" % a])
 
         for t in high[:2]:
             signs(t, 0, 128)
@@ -338,34 +340,45 @@ def rank_program(g, core, T, topo):
         for b in range(4):
             act(T.tb[:, C * b:C * b + C], bank(4 + b, C), F.Copy, ["ps%d" % (4 + b)], ["tb%d" % b], scale=0.5)
         places(0, SH + 1)
-        ts(T.offr[:, SH + 1:NH], T.cnt[:, 255:128 * NV:128], -1.0, 16.0, A.mult, A.add, ["slot%d" % t for t in range(SH + 1, NH)], ["offr"])
+        ts(T.offr[:, SH + 1:NH], T.cnt[:, 255:128 * NV:128], -1.0, pf(12), A.mult, A.add,
+           ["pf12"] + ["slot%d" % t for t in range(SH + 1, NH)], ["offr"])
         places(NH, 16)
         offr = ["offr", "offr0", "offr%d" % NH]
         cp(T.ew[:].indirect(T.offr[:]), T.vrow[:], offr + ["vrow", "vrow1", "ewz"], ["ew"])
-        tp(T.tr[:, 0:160], T.ew[:, 16:176], ["ew"], ["tr0"])
-        tp(T.tr[:, 160:352], T.ew[:, 0:192], ["ew"], ["tr1"])
-        cp(T.offab[:], T.tr[:].indirect(off(LX, 2)), ["tr0", "tr1", "lx"], ["offab"])
+        ts(T.sel[:, 0:16], T.offr[:], pf(12), float(K), A.subtract, A.is_lt, offr, ["sel0"])
+        ts(T.sel[:, 16:32], T.offr[:], pf(12), float(C), A.subtract, A.add, offr, ["sel1"])
+        tp(T.tr[:, 0:K], T.ew[:, 16:16 + K], ["ew"], ["tr0"])
+        tp(T.tr[:, K:2 * K], T.ew[:, 32:32 + K], ["ew"], ["tr1"])
+        tt(T.sel[:, 32:48], T.sel[:, 16:32], T.sel[:, 0:16], A.mult, ["sel0", "sel1"], ["sel2"])
+        cp(T.offab[:, 0:16], T.tr[:].indirect(off(LX, 1)), ["tr0", "tr1", "lx"], ["offa"])
+        cp(T.offab[:, 16:48], T.tr[:].indirect(off(LX + 2, 2)), ["tr0", "tr1", "lx2"], ["offb"])
 
-        ts(T.ah[:, 0:K], T.tp[:, 0:C].indirect(T.offab[:, 0:10]), 0.5, None, A.mult, None, ["tp0", "offab"], ["ah0"])
+        ts(T.ah[:, 0:K], T.tp[:, 0:C].indirect(T.offab[:, 0:10]), 1.0 / 64, None, A.mult, None, ["tp0", "offa"], ["ah0"])
         for b in (1, 2, 3):
-            act(T.ah[:, K * b:K * b + K], T.tp[:, C * b:C * b + C].indirect(T.offab[:, 0:10]), F.Copy,
-                ["tp%d" % b, "offab"], ["ah%d" % b], scale=0.5)
-        for b in (1, 0, 2, 3):
+            act(T.ah[:, K * b:K * b + K], T.tp[:, PW * b:PW * b + C].indirect(T.offab[:, 0:10]), F.Copy,
+                ["tp%d" % b, "offa"], ["ah%d" % b], scale=1.0 / 64)
+        for b in range(4):
+            act(T.te[:, K * b:K * b + K], T.tp[:, PW * b:PW * b + C].indirect(T.offab[:, 32:42]), F.Copy, ["tp%d" % b, "offb"], ["te%d" % b])
+        tt(T.sel[:, 0:16], T.sel[:, 32:48], T.c16[:], A.max, ["sel2", "c16"], ["sel0"])
+        for b in range(4):
             tt(T.zt[:, b:4 * K:4], T.tb[:, C * b:C * b + C].indirect(T.offab[:, 16:26]), T.ah[:, K * b:K * b + K], A.add,
-               ["tb%d" % b, "ah%d" % b, "offab"], ["zt%d" % b])
+               ["tb%d" % b, "ah%d" % b, "offb"], ["zt%d" % b])
+        cp(T.offx[:], T.sel[:, 0:16], ["sel0"], ["offx"])
         qz(T.qz[:], T.sz[:], T.zt[:], ["zt%d" % b for b in range(4)], ["qz"])
         if r == 2:
             qz(T.qv[:], T.sv[:], T.vt[:], ["vt"], ["qv"])
         for b in range(4):
             mm(4 + b, K, T.qw[:, 128 * b:128 * b + 128], T.sw[:, 128 * b:128 * b + 128], T.qz[:], T.sz[:], ["qw", "qz"])
-            act(T.hs[:, HW * b + 16:HW * b + 16 + K], bank(4 + b, K), F.Copy, ["ps%d" % (4 + b)], ["hs%d" % b], scale=0.03125)
-        act(T.g3[:], T.hs[:, HW * 3:HW * 4].indirect(T.offr[:]), F.Copy, ["hs3"] + offr + hz, ["g3"])
-        for b in range(3):
-            tt(T.xs[:, b:1024:4], T.hs[:, HW * b:HW * b + HW].indirect(T.offr[:]), T.tp[:, C * b:C * b + C], A.add,
-               ["hs%d" % b, "tp%d" % b] + offr + hz, ["xs%d" % b])
-        for h in range(2):
-            tt(T.xs[:, 512 * h + 3:512 * h + 512:4], T.g3[:, halves[h]], T.ps[:, 1536 + 128 * h:1664 + 128 * h], A.add, ["g3", "ps3"], ["xs3%d" % h])
-        xt, x_keys = T.xs, [["xs0", "xs1", "xs2", "xs3%d" % h] for h in range(2)]
+            tt(T.tp[:, PW * b + C:PW * b + PW], bank(4 + b, K), T.te[:, K * b:K * b + K], A.add, ["ps%d" % (4 + b), "te%d" % b], ["tu%d" % b])
+        for q, b, hs in (("s", 0, (0, 1)), ("s", 1, (0, 1)), ("s", 2, (1,)), ("v", 2, (0,)), ("v", 3, (0,)), ("v", 3, (1,))):
+            a, e = 128 * hs[0], 128 * hs[-1] + 128
+            out, win = T.xs[:, 4 * a + b:4 * e:4], T.tp[:, PW * b:PW * b + PW].indirect(T.offx[:, a // 16:e // 16])
+            rd, wr = ["tp%d" % b, "tu%d" % b, "offx"], ["xs%d%d" % (b, h) for h in hs]
+            if q == "v":
+                ts(out, win, 0.03125, None, A.mult, None, rd, wr)
+            else:
+                act(out, win, F.Copy, rd, wr, scale=0.03125)
+        xt, x_keys = T.xs, [["xs%d%d" % (b, h) for b in range(4)] for h in range(2)]
 
     for s in SEMAPHORES:
         if s.startswith("snt"):

from concourse.mybir import dt, AluOpType, ActivationFunctionType

A = AluOpType
F = ActivationFunctionType
MASKS = [4, 1, 2]
C, K = 256, 160
SH, NH = 3, 13
NV = NH - SH
SW = C + 1
PW = C + K
X4, BF, F32 = "float8_e4m3fn_x4", "bfloat16", "float32"
SCRATCH = {"ps": ("psum", [128, 4096], F32)}
for _d, _l in (
    (BF, dict(x0=1024, xs=1024, ut=512, vt=512, ones=516, eye=516, ti=1024, tp=4 * PW, tb=1024, ah=4 * K, te=4 * K, zt=4 * K, eqb=C,
              eqs=C, cm=C, mrun=C, mab=32, vrow=C, ew=288, tr=2 * K, cmf=C * NV, cnt=128 * NV, sg=16 * SW, zn=16, d0e=C, d0m=C)),
    (F32, dict(sel=48, c16=16, ssb=288, stw=544, apre=128, sums=C, yy=C, run=C, in4=32, uu=32, in3=C, brep=C, qy=16, acc=32,
               pf=24, i256=C, sq=C, d0x=C, cab=32, yo=C, bs0=16, bs1=16, bs2=16, bl0=16, bl1=16, bl2=16)),
    (X4, dict(qu=128, qv=128, qw=512, qe=512, qz=K, qx0=C, qx1=C, qx2=C, qx3=C, qt0=C, qt1=C, qt2=C, ql0=C, ql1=C, ql2=C)),
    ("uint8", dict(su=128, sv=128, sw=512, se=512, sz=K, sx0=C, sx1=C, sx2=C, sx3=C, st0=C, st1=C, st2=C, sl0=C, sl1=C, sl2=C)),
    ("uint16", dict(offr=16, offx=16, offab=48, offc=72)), ("int32", dict(ic=56, pi=8)),
):
    for _n in _l:
        SCRATCH[_n] = ("sbuf", [128, _l[_n]], _d)
SEMAPHORES = ["nv", "ns", "nt", "ng", "lx", "lx1", "lu", "lv", "lw", "lm", "out"] + [
    "%s%d" % (n, r) for r in range(3) for n in ("arrs", "arrc", "snts", "sntc")]
LB, L6, LAP, L4, LX, LQ = 0, 32, 48, 64, 66, 70


def rank_program(g, core, T, topo):
    rank = T.rank_of(core)
    if rank is None:
        return
    Q = {"v": g.vector, "s": g.scalar, "t": g.tensor, "g": g, "y": g.sync}
    own = {"v": "nv", "s": "ns", "t": "nt", "g": "ng"}
    count = {n: 0 for n in SEMAPHORES}
    seen = {q: {} for q in Q}
    writer, readers = {}, {}
    known = {}

    def wait(q, ev):
        if seen[q].get(ev[0], 0) < ev[1]:
            Q[q].wait_ge(T.sem[ev[0]], ev[1])
            seen[q][ev[0]] = ev[1]
            for s, n in known.get(ev, {}).items():
                seen[q][s] = max(seen[q].get(s, 0), n)

    def before(q, rd, wr):
        me = own.get(q)
        need = {}
        evs = []
        for k in rd:
            if k in writer:
                evs.append(writer[k])
            if k.startswith("ps"):
                evs += [e for e in readers.get(k, []) if e[0] != me]
        for k in wr:
            evs += [e for e in [writer.get(k)] + readers.get(k, []) if e is not None]
        for s, n in evs:
            need[s] = max(need.get(s, 0), n)
        for s in need:
            if not any(known.get((o, need[o]), {}).get(s, 0) >= need[s] for o in need if o != s):
                wait(q, (s, need[s]))

    def after(q, ev, rd, wr):
        known[ev] = dict(seen[q])
        for k in rd:
            readers.setdefault(k, []).append(ev)
        for k in wr:
            writer[k] = ev
            readers[k] = []

    def op(q, rd, wr, f):
        before(q, rd, wr)
        s = own[q]
        f().then_inc(T.sem[s], 1)
        count[s] += 1
        after(q, (s, count[s]), rd, wr)

    def dma(q, s, rd, wr, out, in_):
        before(q, rd, wr)
        Q[q].dma_start(out, in_).then_inc(T.sem[s], 16)
        count[s] += 16
        after(q, (s, count[s]), rd, wr)

    V, S, PE = g.vector, g.scalar, g.tensor

    def off(c, n):
        return T.offc[:, c:c + n]

    def bank(b, n):
        return T.ps[:, 512 * b:512 * b + n]

    def ts(out, in0, s1, s2, o0, o1, rd, wr):
        if o1 is None:
            op("v", rd, wr, lambda: V.tensor_scalar(out, in0, s1, None, o0))
        else:
            op("v", rd, wr, lambda: V.tensor_scalar(out, in0, s1, s2, o0, o1))

    def tt(out, in0, in1, o, rd, wr):
        op("v", rd, wr, lambda: V.tensor_tensor(out, in0, in1, o))

    def cp(out, in_, rd, wr):
        op("v", rd, wr, lambda: V.tensor_copy(out, in_))

    def tp(out, in_, rd, wr):
        op("v", rd, wr, lambda: V.transpose(out, in_))

    def ms(ap, c, wr):
        op("v", [], wr, lambda: V.memset(ap, c))

    def scan(out, d0, d1, o0, o1, rd, wr, first=0.0):
        op("v", rd, wr, lambda: V.tensor_tensor_scan(out, d0, d1, first, o0, o1))

    def qz(q, s, in_, rd, wr):
        op("v", rd, wr, lambda: V.quantize_mx(q, s, in_))

    def act(out, in_, f, rd, wr, **kw):
        op("s", rd, wr, lambda: S.activation(out, in_, f, **kw))

    def mm(b, n, w, ws, x, xs, rd):
        op("t", rd, ["ps%d" % b], lambda: PE.matmul_mx(bank(b, n), w, ws, x, xs, True, True))

    def unpack(b, to, q, s, key):
        mm(to, C, T.qe[:, 128 * b:128 * b + 128], T.se[:, 128 * b:128 * b + 128], q[:], s[:], ["qe%d" % b, key])

    def iota(out, pat, base, cm, wr):
        op("g", [], wr, lambda: g.iota(out, pat, base, cm))

    def pf(i, n=1):
        return T.pf[:, i:i + n]

    def zeros(key, buf, a, b):
        act(buf[:, a:b], T.ones[:, 0:b - a], F.Identity, ["ones"], [key], scale=0.0)

    def units(b):
        qz(T.qe[:, 128 * b:128 * b + 128], T.se[:, 128 * b:128 * b + 128], T.eye[:, 3 - b:515 - b], ["eye"], ["qe%d" % b])

    dma("y", "lx", [], ["x00"], T.x0[:, 0:512], T.x[:, 0:512])
    dma("s", "lu", [], ["ut"], T.ut[:], T.u[:])
    dma("y", "lx1", [], ["x01"], T.x0[:, 512:1024], T.x[:, 512:1024])
    ms(T.ones[:], 1.0, ["ones"])
    iota(T.pi[:, 0:1], [[1, 1]], 0, 1, ["p"])
    iota(T.ic[:, 0:16], [[1, 16]], 0, 0, ["ic0"])
    op("g", [], ["i256"], lambda: g.iota(T.i256[:], [[0, 16], [1, 16]], 0, 0, allow_small_or_imprecise_dtypes=True))
    op("g", ["ones"], ["eye"], lambda: g.affine_select(T.eye[:], T.ones[:], [[-1, 516]], A.is_equal, 0.0, 3, 4))
    iota(T.ic[:, 16:24], [[0, 4], [16, 2]], 0, 0, ["ic1"])
    iota(T.ic[:, 32:48], [[2, 8], [16, 2]], 0, 0, ["ic2"])
    iota(T.ic[:, 48:50], [[0, 2]], 15, 16, ["ic3"])
    zeros("ewz", T.ew, 16, 32)
    zeros("ssbe", T.ssb, 0, 16)
    zeros("ssbe2", T.ssb, 272, 288)
    ts(T.pi[:, 1:2], T.pi[:, 0:1], 15, None, A.bitwise_and, None, ["p"], ["p1"])
    ts(T.pi[:, 2:3], T.pi[:, 0:1], 4, 1, A.logical_shift_right, A.bitwise_and, ["p"], ["p2"])
    ts(T.pi[:, 3:4], T.pi[:, 0:1], 1, None, A.bitwise_and, None, ["p"], ["p3"])
    ts(T.pi[:, 4:5], T.pi[:, 0:1], 31, None, A.bitwise_and, None, ["p"], ["p4"])
    ms(T.zn[:], 0.0, ["zn0"])
    cp(off(LB, 16), T.ic[:, 0:16], ["ic0"], ["lb"])
    cp(pf(0, 4), T.pi[:, 0:4], ["p", "p1", "p2", "p3"], ["pf"])
    R, H, R0 = pf(1), pf(2), pf(3)
    cp(off(LQ, 1), T.pi[:, 4:5], ["p4"], ["lq"])
    ts(T.cab[:, 16:32], T.ic[:, 0:16], 16.0, None, A.mult, None, ["ic0"], ["conb"])
    tt(pf(6), R0, H, A.not_equal, ["pf"], ["par"])
    ts(pf(7), R, H, 16.0, A.subtract, A.mult, ["pf"], ["pf7"])
    ts(pf(10), R, 9.0, 16.0, A.min, A.mult, ["pf"], ["pf10"])
    ts(pf(20), R, 16.0, None, A.mult, None, ["pf"], ["pf20"])
    ts(pf(8), pf(6), 272.0, pf(7), A.mult, A.add, ["par", "pf7"], ["pf8"])
    ts(pf(12), H, 16.0, 16.0, A.mult, A.add, ["pf"], ["pf12"])
    ts(pf(11), R0, 144.0, pf(10), A.mult, A.add, ["pf", "pf10"], ["pf11"])
    ts(T.cab[:, 0:16], T.zn[:], pf(20), None, A.add, None, ["zn0", "pf20"], ["cona"])
    act(T.d0m[:], T.i256[:], F.Sign, ["i256"], ["d0m"])
    act(T.sq[:], T.i256[:], F.Square, ["i256", "pf"], ["sq"], bias=R, scale=-1.0)
    act(T.d0x[:], T.d0m[:], F.Identity, ["d0m"], ["d0x"], bias=-1.0e29, scale=1.0e29)
    act(T.d0e[:], T.sq[:], F.Sign, ["sq"], ["d0e"])
    qz(T.qu[:], T.su[:], T.ut[:], ["ut"], ["qu"])

    def late_constants():
        ts(T.ic[:, 50:52], T.ic[:, 48:50], 255, None, A.bitwise_and, None, ["ic3"], ["ic4"])
        ts(off(L6, 16), T.ic[:, 32:48], H, None, A.add, None, ["ic2", "pf"], ["l6"])
        cp(off(L4, 2), T.ic[:, 50:52], ["ic4"], ["l4"])

    halves = [slice(0, 128), slice(128, C)]
    xt, x_keys = T.x0, [["x00"], ["x01"]]
    for r in range(3):
        mate = T.cores[rank ^ MASKS[r]]
        rid, pid = topo.addr(mate, core)
        eng = topo.engines(core, mate)
        qx, sx, qt, st = T["qx%d" % r], T["sx%d" % r], T["qt%d" % r], T["st%d" % r]
        ql, sl, bs, bl = T["ql%d" % r], T["sl%d" % r], T["bs%d" % r], T["bl%d" % r]

        def send(out, in_, es, arr, snt, rd):
            before("g", rd, [])
            g.remote_dma(out, in_, T.sem[arr], T.sem[snt], pid, rid, sum(1 << e for e in es))
            count[arr] += len(es)
            count[snt] += len(es)

        for h in range(2):
            c = halves[h]
            qz(qx[:, c], sx[:, c], xt[:, 512 * h:512 * h + 512], x_keys[h], ["qx%d%d" % (r, h)])
            mm(6 + h, 128, T.qu[:], T.su[:], qx[:, c], sx[:, c], ["qu", "qx%d%d" % (r, h)])
        writer["qx%d" % r] = writer["qx%d1" % r]
        if r == 0:
            ts(pf(13), pf(11), pf(12), -16.0, A.add, A.add, ["pf11", "pf12"], ["pf13"])
            ts(T.c16[:], T.cab[:, 16:32], R, None, A.add, None, ["conb", "pf"], ["c16"])
        for h in range(2):
            tp(T.stw[:, halves[h]], bank(6 + h, 128), ["ps%d" % (6 + h)], ["stw%d" % h])
        if r == 0:
            cp(off(LX, 1), pf(13), ["pf13"], ["lx"])
            ts(off(LX + 2, 2), T.ic[:, 1:3], pf(13), None, A.add, None, ["ic0", "pf13"], ["lx2"])
        cp(bs[:], T.stw[:, 1:256:16], ["stw0", "stw1"], ["bs%d" % r])
        send(bl[:], bs[:], eng[:8], "arrs%d" % r, "snts%d" % r, ["bs%d" % r])
        writer["bl"] = ("arrs%d" % r, count["arrs%d" % r])
        if r == 0:
            op("g", [], ["vrow"], lambda: g.iota(T.vrow[:], [[1, C]], 0, 0, allow_small_or_imprecise_dtypes=True))
            ts(off(LAP, 8), T.ic[:, 16:24], pf(8), None, A.add, None, ["ic1", "pf8"], ["lap"])
            units(2)
        for h in range(2):
            act(T.ssb[:, 16 + 128 * h:144 + 128 * h], bank(6 + h, 128), F.Copy, ["ps%d" % (6 + h)], ["ssb%d" % h])
        tp(T.stw[:, 256:544], T.ssb[:], ["ssb0", "ssb1", "ssbe", "ssbe2"], ["stw2"])
        for b in (2, 0, 1, 3):
            if r == 0 and b != 2:
                units(b)
            unpack(b, b, qx, sx, "qx%d" % r)
        act(T.apre[:], T.stw[:].indirect(off(LAP, 8)), F.Copy, ["stw0", "stw1", "stw2", "lap"], ["apre"])
        cp(T.ti[:, 2:1024:4], bank(2, C), ["ps2"], ["ti2"])
        for b in (0, 1, 3):
            act(T.ti[:, b:1024:4], bank(b, C), F.Copy, ["ps%d" % b], ["ti%d" % b])

        def requantise(h):
            qz(qt[:, halves[h]], st[:, halves[h]], T.ti[:, 512 * h:512 * h + 512], ["ti%d" % b for b in range(4)], ["qt%d%d" % (r, h)])
            if h == 1:
                keys = ["qt%d0" % r, "qt%d1" % r]
                send(ql[:].bitcast(dt.uint8), qt[:].bitcast(dt.uint8), eng, "arrc%d" % r, "sntc%d" % r, keys)
                send(sl[:], st[:], eng, "arrc%d" % r, "sntc%d" % r, keys)
                writer["ql"] = ("arrc%d" % r, count["arrc%d" % r])
                for b in range(4):
                    unpack(b, 4 + b, ql, sl, "ql")

        def plane(b):
            act(T.tp[:, PW * b:PW * b + C], T.ti[:, b:1024:4], F.Copy, ["ti%d" % b], ["tp%d" % b], scale=32.0)

        if r == 0:
            late_constants()
        plane(0)
        plane(1)

        for h in range(2):
            tt(T.sums[:, halves[h]], bl[:].indirect(off(LB + 8 * h, 8)), T.apre[:], A.add, ["bl", "lb", "apre"], ["sums%d" % h])
        for h in range(2):
            tp(T.yy[:, halves[h]], T.sums[:, halves[h]], ["sums%d" % h], ["yy%d" % h])
        for h in range(2):
            scan(T.run[:, halves[h]], T.d0x[:, halves[h]], T.yy[:, halves[h]], A.add, A.max, ["d0x", "yy%d" % h], ["run%d" % h])
        requantise(0)
        cp(T.in4[:, 0:16], T.run[:, 15:C:16], ["run0", "run1"], ["in4"])
        act(T.in4[:, 16:32], T.run[:, 15:C:16], F.Copy, ["run0", "run1"], ["in4b"])
        requantise(1)
        tp(T.uu[:], T.in4[:], ["in4", "in4b"], ["uu"])
        for h in range(2):
            act(T.in3[:, halves[h]], T.uu[:].indirect(off(L6 + 8 * h, 8)), F.Copy, ["uu", "l6"], ["in3%d" % h])
        act(T.qy[:], T.uu[:].indirect(off(LQ, 1)), F.Copy, ["uu", "lq"], ["qy"])
        tt(T.cm[:], T.in4[:, 0:16].indirect(off(LB, 16)), T.run[:], A.is_gt, ["in4", "run0", "run1", "lb"], ["cm"])
        tp(T.brep[:, halves[0]], T.in3[:, halves[0]], ["in30"], ["brep0"])
        scan(T.mrun[:], T.d0m[:], T.cm[:], A.mult, A.add, ["d0m", "cm"], ["mrun"])
        tp(T.brep[:, halves[1]], T.in3[:, halves[1]], ["in31"], ["brep"])

        low, high = list(range(SH)), list(range(15, NH - 1, -1))

        def signs(t, a, b):
            act(T.sg[:, SW * t + a:SW * t + b], T.brep[:, a:b], F.Sign, ["brep0" if b <= 128 else "brep", "qy"],
                ["sg%d" % t, "sa%d" % t, "sb%d" % t], bias=T.qy[:, t:t + 1], scale=-1.0)

        def left(t):
            w = T.sg[:, SW * t:SW * t + 16 * t + 16]
            act(w, w, F.Sign, ["sg%d" % t], ["sa%d" % t], bias=1.0, scale=-1.0, accum_out=T.acc[:, t:t + 1])

        def right(t):
            w = T.sg[:, SW * t + 16 * t + 15:SW * t + C] if t == SH else T.sg[:, SW * t + 16 * t + 16:SW * t + SW]
            act(w, w, F.Relu, ["sg%d" % t, "slot%d" % t], ["sb%d" % t], scale=-1.0, accum_out=T.acc[:, 16 + t:17 + t])

        def whole(t, sides=(0, 1)):
            for side in sides:
                a, b, c = (0, 16 * t + 16, A.is_ge) if side == 0 else (16 * t + 16, C, A.is_gt)
                o = C * (t - SH)
                ts(T.cmf[:, o + a:o + b], T.brep[:, a:b], T.qy[:, t:t + 1], -1.0, c, A.mult, ["brep", "qy"], ["f%d_%d" % (t, side)])

        def total(t):
            o, w = C * (t - SH), 8 * t + 8 if t == SH else 128
            out = T.sg[:, SW * t + w:SW * t + 2 * w] if t == SH else T.cnt[:, 128 * (t - SH):128 * (t - SH) + 128]
            scan(out, T.cmf[:, o:o + w], T.cmf[:, o + w:o + 2 * w], A.add, A.add, ["f%d_0" % t, "f%d_1" % t, "eqs"],
                 ["slot%d" % t], first=T.eqs[:, 16 * t + 15:16 * t + 16])

        def slots(a, b):
            tt(T.sg[:, SW * a + C:SW * b:SW], T.eqs[:, 16 * a + 15:16 * b:16], T.acc[:, a:b], A.subtract,
               ["eqs"] + ["sa%d" % t for t in range(a, b)], ["slot%d" % t for t in range(a, b)])

        def places(a, b):
            ts(T.offr[:, a:b], T.acc[:, 16 + a:16 + b], pf(12), None, A.add, None, ["pf12"] + ["sb%d" % t for t in range(a, b)], ["offr%d" % a])

        for t in high[:2]:
            signs(t, 0, 128)
        for t in low + high[2:]:
            signs(t, 0, C)
        for t in low:
            left(t)
        for t in high[:2]:
            signs(t, 128, C)
        signs(SH, 16 * SH + 16, C)
        for t in high[2:] + high[:2]:
            left(t)

        tt(T.mab[:], T.mrun[:].indirect(off(L4, 2)), T.cab[:], A.add, ["mrun", "l4", "cona", "conb"], ["mab"])
        for y in range(2):
            dma("y", "lm", ["mab"], ["vrow"] if y == 0 else ["vrow1"], T.vrow[y:128:16, :], T.mab[:, 16 * y:16 * y + 16])
        writer["vrow"] = writer["vrow1"]
        readers["mab"] = [writer["vrow"]]
        if r == 0:
            wait("y", ("sntc0", count["sntc0"]))
            dma("y", "lw", [], [], T.qw[:].bitcast(dt.uint8), T.wc[:])
            dma("y", "lw", [], ["qw"], T.sw[:], T.ws[:])
        if r == 1:
            dma("y", "lv", [], ["vt"], T.vt[:], T.v[:])
        tt(T.eqb[:], T.qy[:].indirect(off(LB, 16)), T.brep[:], A.is_equal, ["qy", "lb", "brep"], ["eqb"])
        whole(SH + 1)
        scan(T.eqs[:], T.d0e[:], T.eqb[:], A.mult, A.add, ["d0e", "eqb"], ["eqs"])
        whole(SH, (0,))
        for t in range(SH + 2, NH):
            whole(t)
            if t == NH - 4:
                slots(0, SH)
                total(SH)
        for t in low + [SH]:
            right(t)
        for t in range(SH + 1, NH):
            if t == SH + 3:
                slots(NH, 16)
            total(t)
        for t in high:
            right(t)
        plane(2)
        plane(3)
        for b in range(4):
            act(T.tb[:, C * b:C * b + C], bank(4 + b, C), F.Copy, ["ps%d" % (4 + b)], ["tb%d" % b], scale=0.5)
        places(0, SH + 1)
        ts(T.offr[:, SH + 1:NH], T.cnt[:, 255:128 * NV:128], -1.0, pf(12), A.mult, A.add,
           ["pf12"] + ["slot%d" % t for t in range(SH + 1, NH)], ["offr"])
        places(NH, 16)
        offr = ["offr", "offr0", "offr%d" % NH]
        cp(T.ew[:].indirect(T.offr[:]), T.vrow[:], offr + ["vrow", "vrow1", "ewz"], ["ew"])
        ts(T.sel[:, 0:16], T.offr[:], pf(12), float(K), A.subtract, A.is_lt, offr, ["sel0"])
        ts(T.sel[:, 16:32], T.offr[:], pf(12), float(C), A.subtract, A.add, offr, ["sel1"])
        tp(T.tr[:, 0:K], T.ew[:, 16:16 + K], ["ew"], ["tr0"])
        tp(T.tr[:, K:2 * K], T.ew[:, 32:32 + K], ["ew"], ["tr1"])
        tt(T.sel[:, 32:48], T.sel[:, 16:32], T.sel[:, 0:16], A.mult, ["sel0", "sel1"], ["sel2"])
        cp(T.offab[:, 0:16], T.tr[:].indirect(off(LX, 1)), ["tr0", "tr1", "lx"], ["offa"])
        cp(T.offab[:, 16:48], T.tr[:].indirect(off(LX + 2, 2)), ["tr0", "tr1", "lx2"], ["offb"])

        ts(T.ah[:, 0:K], T.tp[:, 0:C].indirect(T.offab[:, 0:10]), 1.0 / 64, None, A.mult, None, ["tp0", "offa"], ["ah0"])
        for b in (1, 2, 3):
            act(T.ah[:, K * b:K * b + K], T.tp[:, PW * b:PW * b + C].indirect(T.offab[:, 0:10]), F.Copy,
                ["tp%d" % b, "offa"], ["ah%d" % b], scale=1.0 / 64)
        for b in range(4):
            act(T.te[:, K * b:K * b + K], T.tp[:, PW * b:PW * b + C].indirect(T.offab[:, 32:42]), F.Copy, ["tp%d" % b, "offb"], ["te%d" % b])
        tt(T.sel[:, 0:16], T.sel[:, 32:48], T.c16[:], A.max, ["sel2", "c16"], ["sel0"])
        for b in range(4):
            tt(T.zt[:, b:4 * K:4], T.tb[:, C * b:C * b + C].indirect(T.offab[:, 16:26]), T.ah[:, K * b:K * b + K], A.add,
               ["tb%d" % b, "ah%d" % b, "offb"], ["zt%d" % b])
        cp(T.offx[:], T.sel[:, 0:16], ["sel0"], ["offx"])
        qz(T.qz[:], T.sz[:], T.zt[:], ["zt%d" % b for b in range(4)], ["qz"])
        if r == 2:
            qz(T.qv[:], T.sv[:], T.vt[:], ["vt"], ["qv"])
        for b in range(4):
            mm(4 + b, K, T.qw[:, 128 * b:128 * b + 128], T.sw[:, 128 * b:128 * b + 128], T.qz[:], T.sz[:], ["qw", "qz"])
            tt(T.tp[:, PW * b + C:PW * b + PW], bank(4 + b, K), T.te[:, K * b:K * b + K], A.add, ["ps%d" % (4 + b), "te%d" % b], ["tu%d" % b])
        for q, b, hs in (("s", 0, (0, 1)), ("s", 1, (0, 1)), ("s", 2, (1,)), ("v", 2, (0,)), ("v", 3, (0,)), ("v", 3, (1,))):
            a, e = 128 * hs[0], 128 * hs[-1] + 128
            out, win = T.xs[:, 4 * a + b:4 * e:4], T.tp[:, PW * b:PW * b + PW].indirect(T.offx[:, a // 16:e // 16])
            rd, wr = ["tp%d" % b, "tu%d" % b, "offx"], ["xs%d%d" % (b, h) for h in hs]
            if q == "v":
                ts(out, win, 0.03125, None, A.mult, None, rd, wr)
            else:
                act(out, win, F.Copy, rd, wr, scale=0.03125)
        xt, x_keys = T.xs, [["xs%d%d" % (b, h) for b in range(4)] for h in range(2)]

    for s in SEMAPHORES:
        if s.startswith("snt"):
            wait("y", (s, count[s]))
    for h in range(2):
        c = halves[h]
        qz(T.qx3[:, c], T.sx3[:, c], xt[:, 512 * h:512 * h + 512], x_keys[h], ["qx3%d" % h])
        mm(4 + h, 128, T.qv[:], T.sv[:], T.qx3[:, c], T.sx3[:, c], ["qv", "qx3%d" % h])
    writer["qx3"] = writer["qx31"]
    dma("y", "out", ["qx3"], [], T.oc[:], T.qx3[:].bitcast(dt.uint8))
    for k in range(4):
        dma("ys"[k % 2], "out", ["qx3"], [], T.osc[4 * k:4 * k + 4, :], T.sx3[32 * k:32 * k + 4, :])
    cp(T.yo[:, 0:128], bank(4, 128), ["ps4"], ["yo0"])
    cp(T.yo[:, 128:256], bank(5, 128), ["ps5"], ["yo1"])
    dma("s", "out", ["yo0", "yo1"], [], T.y[:], T.yo[:])
    for s in SEMAPHORES:
        if all(seen[q].get(s, 0) < count[s] for q in Q):
            wait("y", (s, count[s]))
